import numpy as np
import ml_dtypes


def mxq(x, axis, fmt="e4m3"):
    dtype, down = {"e4m3": (ml_dtypes.float8_e4m3fn, 7), "e5m2": (ml_dtypes.float8_e5m2, 14)}[fmt]
    v = np.moveaxis(np.asarray(x, np.float32).astype(ml_dtypes.bfloat16).astype(np.float64), axis, -1)
    blocks = v.reshape(v.shape[:-1] + (-1, 32))
    amax = np.abs(blocks).max(-1, keepdims=True)
    byte = np.maximum(np.where(amax > 0, np.frexp(amax)[1] - 1 + 127, 0) - down, 1)
    scale = np.exp2(byte - 127.0)
    codes = (blocks / scale).astype(np.float32).astype(dtype).astype(np.float64)
    return np.moveaxis((codes * scale).reshape(v.shape), -1, axis)


WIDE = False


def mx_kscale(k):
    if not WIDE:
        return np.ones(k)
    levels = np.array([10, -10, 5, -5, 0])
    if k % 512:
        return np.exp2(np.random.permutation(np.resize(levels, k // 32))).repeat(32)
    a = np.empty((k // 512, 16))
    for p in range(k // 512):
        a[p, :8] = np.random.permutation(np.resize(levels, 8))
        for g in range(8):
            far = levels[np.abs(levels - a[p, g]) >= 10]
            a[p, g + 8] = far[np.random.randint(len(far))]
    return np.exp2(a.ravel()).repeat(32)


def f64(x):
    return np.asarray(x).astype(np.float64)


def striped(idx):
    return np.tile(np.asarray(idx).reshape(-1, 16).T, (8, 1)).astype(np.uint16)


def unstriped(offs):
    return offs[:16].T.reshape(-1).astype(np.int64)


E2M1 = np.array([0.0, 0.5, 1.0, 1.5, 2.0, 3.0, 4.0, 6.0, -0.0, -0.5, -1.0, -1.5, -2.0, -3.0, -4.0, -6.0])


def pack_weight(w, fmt):
    k, n = w.shape
    w = f64(np.asarray(w, np.float32).astype(ml_dtypes.bfloat16)).reshape(k // 32, 32, n)
    amax = np.abs(w).max(1)
    if fmt == "e4m3":
        byte = np.frexp(amax)[1] - 1 + 127 - 7
    else:
        mant, ex = np.frexp(amax / 6.0)
        byte = np.where(mant > 0.5, ex, ex - 1) + 127
    byte = np.clip(np.where(amax > 0, byte, 1), 1, 254)
    scaled = (w * np.exp2(127.0 - byte)[:, None, :]).reshape(k, n).astype(np.float32)
    by_word = np.ascontiguousarray(scaled.reshape(k // 512, 128, 4, n).transpose(0, 1, 3, 2))
    if fmt == "e4m3":
        words = by_word.astype(ml_dtypes.float8_e4m3fn).view(np.uint8)
    else:
        c = by_word.astype(ml_dtypes.float4_e2m1fn).view(np.uint8) & 0xF
        words = (c[..., 0::2] | (c[..., 1::2] << 4)).reshape(k // 512, 128, 2 * n)
    return np.ascontiguousarray(words), np.ascontiguousarray(byte.astype(np.uint8).reshape(k // 512, 16, n))


def unpack_weight(words, scales, fmt):
    g, _, n = scales.shape
    words = np.ascontiguousarray(words).reshape(g, 128, n, -1)
    if fmt == "e4m3":
        vals = words.view(ml_dtypes.float8_e4m3fn).astype(np.float64)
    else:
        nib = np.empty((g, 128, n, 4), np.uint8)
        nib[..., 0::2] = words & 0xF
        nib[..., 1::2] = words >> 4
        vals = E2M1[nib]
    vals = vals * np.repeat(np.exp2(scales.astype(np.float64) - 127.0), 8, axis=1)[..., None]
    return vals.transpose(0, 1, 3, 2).reshape(g * 512, n)


def gelu(v):
    return 0.5 * v * (1.0 + np.tanh(0.7978845608028654 * (v + 0.044715 * v ** 3)))


K, T, J, F, D = 512, 2048, 512, 512, 256


def setup_inputs():
    n = np.random.standard_normal
    idx = np.random.permutation(T)[:J]
    idx2 = np.random.permutation(T)[:J]
    idx3 = np.random.permutation(T)[:J]
    idx4 = np.random.permutation(T)[:J]
    fk = mx_kscale(K)
    ff = mx_kscale(F)
    tokp = pack_weight(n((K, T)) / fk[:, None], "e2m1")
    return {
        "tok_words": tokp[0],
        "tok_scales": tokp[1],
        "w0": (n((K, F)) * 0.5 / np.sqrt(K) * fk[:, None]).astype(np.float32),
        "w1": (n((K, F)) * 0.5 / np.sqrt(K) * fk[:, None]).astype(np.float32),
        "w2": (n((K, F)) * 0.5 / np.sqrt(K) * fk[:, None]).astype(np.float32),
        "w3": (n((K, F)) * 0.5 / np.sqrt(K) * fk[:, None]).astype(np.float32),
        "gain": (np.random.uniform(0.5, 2.0, (F, 1)) * ff[:, None]).astype(np.float32),
        "wo": (n((F, D)) * 1 / np.sqrt(F) / ff[:, None]).astype(np.float32),
        "offs": striped(idx),
        "offs2": striped(idx2),
        "offs3": striped(idx3),
        "offs4": striped(idx4),
    }


def reference(tok_words, tok_scales, w0, w1, w2, w3, gain, wo, offs, offs2, offs3, offs4):
    idx = unstriped(offs)
    idx2 = unstriped(offs2)
    idx3 = unstriped(offs3)
    idx4 = unstriped(offs4)
    toku = unpack_weight(tok_words, tok_scales, "e2m1")
    w0q = mxq(f64(w0), 0, "e4m3")
    tokidxg = toku[:, idx]
    w1q = mxq(f64(w1), 0, "e4m3")
    tokidx2g = toku[:, idx2]
    w2q = mxq(f64(w2), 0, "e4m3")
    tokidx3g = toku[:, idx3]
    w3q = mxq(f64(w3), 0, "e4m3")
    tokidx4g = toku[:, idx4]
    z = w0q.T @ tokidxg + w1q.T @ tokidx2g + w2q.T @ tokidx3g + w3q.T @ tokidx4g
    g = gelu(z) * f64(gain)
    woq = mxq(f64(wo), 0, "e4m3")
    gq = mxq(g, 0, "e4m3")
    y = woq.T @ gq
    return y

@@ -1,0 +1,173 @@
+from contextlib import ExitStack
+
+import concourse.mybir as mybir
+from concourse.masks import make_identity
+
+K, T, J, F, D = 512, 2048, 512, 512, 256
+P = 128
+PACK = 4
+PLACES = 4
+FLOPS = 2 * PLACES * K * F * J + 2 * F * D * J
+
+F32 = mybir.dt.float32
+BF16 = mybir.dt.bfloat16
+I32 = mybir.dt.int32
+U32 = mybir.dt.uint32
+U16 = mybir.dt.uint16
+U8 = mybir.dt.uint8
+FP8X4 = mybir.dt.float8_e4m3fn_x4
+FP4X4 = mybir.dt.float4_e2m1fn_x4
+GELU = mybir.ActivationFunctionType.Gelu_apprx_tanh
+MULT = mybir.AluOpType.mult
+
+
+def tile_attend_nsa_compress_kernel(tc, tok_words, tok_scales, w0, w1, w2, w3, gain, wo, offs, offs2, offs3, offs4, out):
+    nc = tc.nc
+    weights = (w0, w1, w2, w3)
+    lists = (offs, offs2, offs3, offs4)
+    with ExitStack() as ctx:
+        keep = ctx.enter_context(tc.tile_pool(name="keep", bufs=1))
+        psum = ctx.enter_context(tc.psum_pool(name="psum", bufs=1))
+
+        pool_words = keep.tile([P, T], U16, name="pool_words", align_bytes=64)
+        pool_scales = keep.tile([P, T], U8, name="pool_scales", align_bytes=64)
+        offsets = [keep.tile([P, J // 16], U16, name="offsets%d" % i) for i in range(PLACES)]
+
+        def load_columns(name, w, cols):
+            width = cols.stop - cols.start
+            raw = keep.tile([P, PACK, width], F32, name=name, tag=name, align_bytes=64)
+            nc.sync.dma_start(out=raw[:], in_=w.rearrange("(p r) c -> p r c", r=PACK)[:, :, cols])
+            return raw
+
+        def cast(raw, grouped, cols):
+            nc.scalar.copy(
+                out=grouped[:, cols, :].rearrange("p (c i) r -> p c r i", i=4),
+                in_=raw[:].rearrange("p r (c i) -> p c r i", i=4),
+            )
+
+        def planes(name, width):
+            codes = keep.tile([P, width], U32, name=name + "_codes", align_bytes=64)
+            scales = keep.tile([P, width], U8, name=name + "_scales", align_bytes=64)
+            return codes, scales
+
+        def quantise(codes, scales, grouped, cols):
+            nc.vector.quantize_mx(out=codes[:, cols].bitcast(FP8X4), scales=scales[:, cols], in_=grouped[:, cols, :].rearrange("p c r -> p (c r)"))
+
+        def gather(name, window, dtype, place, tag, first=0, count=J):
+            picked = keep.tile([P, count], dtype, name=name, tag=tag, align_bytes=64)
+            nc.vector.tensor_copy(out=picked[:], in_=window[:].indirect(offsets[place][:, first // 16 : (first + count) // 16]))
+            return picked
+
+        halves = (slice(0, F // 2), slice(F // 2, F))
+        whole = slice(0, F)
+
+        nc.vector.memset(pool_scales[:].bitcast(I32), 0)
+        nc.sync.dma_start(offsets[0][:], lists[0])
+        nc.sync.dma_start(out=pool_words[:].bitcast(I32), in_=tok_words[0].bitcast(I32))
+        for q in range(4):
+            nc.sync.dma_start(
+                out=pool_scales[32 * q : 32 * q + 4, :].bitcast(I32),
+                in_=tok_scales[0, 4 * q : 4 * q + 4, :].bitcast(I32),
+            )
+        nc.sync.dma_start(offsets[1][:], lists[1])
+        raw = {}
+        for i in range(PLACES):
+            for u in range(2):
+                raw[i, u] = load_columns("raw%d%d" % (i, u), weights[i], halves[u])
+                if i == 1:
+                    nc.sync.dma_start(offsets[2 + u][:], lists[2 + u])
+        raw_wo = load_columns("raw_wo", wo, slice(0, D))
+        gains = keep.tile([P, PACK], F32, name="gains")
+        nc.sync.dma_start(out=gains[:], in_=gain.rearrange("(p r) o -> p (r o)", r=PACK))
+
+        warm = keep.tile([P, 2], F32, name="warm")
+        nc.vector.memset(warm[:, 0:1], 0.0)
+        warm_out = keep.tile([P, 1], F32, name="warm_out")
+        nc.scalar.activation(out=warm_out[:], in_=warm[:, 0:1], func=GELU)
+        identity = keep.tile([P, P], F32, name="identity")
+        make_identity(nc, identity[:])
+
+        grouped = [keep.tile([P, F, PACK], BF16, name="grouped%d" % i, tag="grouped%d" % i, align_bytes=64) for i in range(PLACES)]
+        wq = [planes("w%d" % i, F) for i in range(PLACES)]
+        z = [psum.tile([P, F], F32, name="z%d" % b) for b in range(J // P)]
+
+        def multiply(place, words, scales, blocks):
+            for n, b in enumerate(blocks):
+                cols = slice(n * P, (n + 1) * P)
+                nc.tensor.matmul_mx(
+                    out=z[b][:],
+                    lhsT=words[:, cols].bitcast(FP4X4),
+                    lhsT_scale=scales[:, cols],
+                    rhs=wq[place][0][:].bitcast(FP8X4),
+                    rhs_scale=wq[place][1][:],
+                    start=(place == 0),
+                    stop=(place == PLACES - 1),
+                )
+
+        def both_halves(place):
+            for u in range(2):
+                cast(raw[place, u], grouped[place], halves[u])
+            quantise(*wq[place], grouped[place], whole)
+
+        words0 = gather("words0", pool_words, U16, 0, "words0")
+        words1 = gather("words1", pool_words, U16, 1, "words1")
+        scales0 = gather("scales0", pool_scales, U8, 0, "scales0")
+        both_halves(0)
+        multiply(0, words0, scales0, range(4))
+        scales1 = gather("scales1", pool_scales, U8, 1, "raw01")
+        both_halves(1)
+        multiply(1, words1, scales1, range(4))
+        words2 = gather("words2", pool_words, U16, 2, "raw10")
+        scales2 = gather("scales2", pool_scales, U8, 2, "raw11")
+        both_halves(2)
+        multiply(2, words2, scales2, range(4))
+        words3a = gather("words3a", pool_words, U16, 3, "raw21", 0, J // 2)
+        cast(raw[3, 0], grouped[3], halves[0])
+        quantise(*wq[3], grouped[3], halves[0])
+        scales3a = gather("scales3a", pool_scales, U8, 3, "raw30", 0, J // 2)
+        cast(raw[3, 1], grouped[3], halves[1])
+        quantise(*wq[3], grouped[3], halves[1])
+        multiply(3, words3a, scales3a, (0, 1))
+        words3b = gather("words3b", pool_words, U16, 3, "raw31", J // 2, J // 2)
+        scales3b = gather("scales3b", pool_scales, U8, 3, "grouped3", J // 2, J // 2)
+        grouped_wo = keep.tile([P, D, PACK], BF16, name="grouped_wo", align_bytes=64)
+        cast(raw_wo, grouped_wo, slice(0, D))
+        wo_codes, wo_scales = planes("wo", D)
+        quantise(wo_codes, wo_scales, grouped_wo, slice(0, D))
+
+        out_rows = out.rearrange("(h p) j -> p h j", p=P)
+        for b in range(J // P):
+            if b == 1:
+                multiply(3, words3b, scales3b, (2, 3))
+            act = keep.tile([P, PACK, P], F32, name="act%d" % b)
+            dealt = z[b][:].rearrange("p (m t) -> p t m", t=PACK)
+            step = 2 if b == 0 else PACK
+            for t in range(0, PACK, step):
+                nc.scalar.activation(out=act[:, t : t + step, :], in_=dealt[:, t : t + step, :], func=GELU)
+            turned = psum.tile([P, PACK, P], F32, name="turned%d" % b, tag="turned", bufs=2)
+            for t in range(PACK):
+                nc.tensor.transpose(turned[:, t, :], act[:, t, :], identity[:])
+            g = keep.tile([P, P, PACK], BF16, name="g%d" % b, align_bytes=64)
+            nc.vector.tensor_tensor(
+                out=g[:],
+                in0=turned[:].rearrange("p t j -> p j t"),
+                in1=gains[:].unsqueeze(1).to_broadcast([P, P, PACK]),
+                op=MULT,
+            )
+            g_codes, g_scales = planes("g%d" % b, P)
+            quantise(g_codes, g_scales, g, slice(0, P))
+            y = psum.tile([P, D // P, P], F32, name="y%d" % b, tag="y", bufs=2)
+            for h in range(D // P):
+                cols = slice(h * P, (h + 1) * P)
+                nc.tensor.matmul_mx(
+                    out=y[:, h, :],
+                    lhsT=wo_codes[:, cols].bitcast(FP8X4),
+                    lhsT_scale=wo_scales[:, cols],
+                    rhs=g_codes[:].bitcast(FP8X4),
+                    rhs_scale=g_scales[:],
+                    start=True,
+                    stop=True,
+                )
+            result = keep.tile([P, D // P, P], F32, name="result%d" % b)
+            nc.scalar.copy(out=result[:], in_=y[:])
+            nc.sync.dma_start(out=out_rows[:, :, b * P : (b + 1) * P], in_=result[:])

@@ -1,12 +1,12 @@
 from contextlib import ExitStack
 
 import concourse.mybir as mybir
-from concourse.masks import make_identity
 
 K, T, J, F, D = 512, 2048, 512, 512, 256
 P = 128
 PACK = 4
 PLACES = 4
+SPLIT = 128
 FLOPS = 2 * PLACES * K * F * J + 2 * F * D * J
 
 F32 = mybir.dt.float32
@@ -39,10 +39,17 @@ def tile_attend_nsa_compress_kernel(tc, tok_words, tok_scales, w0, w1, w2, w3, g
             nc.sync.dma_start(out=raw[:], in_=w.rearrange("(p r) c -> p r c", r=PACK)[:, :, cols])
             return raw
 
-        def cast(raw, grouped, cols):
-            nc.scalar.copy(
-                out=grouped[:, cols, :].rearrange("p (c i) r -> p c r i", i=4),
-                in_=raw[:].rearrange("p r (c i) -> p c r i", i=4),
+        def cast(raw, grouped, copy):
+            copy(
+                out=grouped.rearrange("p (c i) r -> p c r i", i=4),
+                in_=raw.rearrange("p r (c i) -> p c r i", i=4),
+            )
+
+        def cast_dealt(raw, grouped, first, copy):
+            m = slice(first, first + raw.shape[2] // PACK)
+            copy(
+                out=grouped[:, :, m, :].rearrange("p t m r -> p m r t"),
+                in_=raw.rearrange("p r (m t) -> p m r t", t=PACK),
             )
 
         def planes(name, width):
@@ -50,24 +57,24 @@ def tile_attend_nsa_compress_kernel(tc, tok_words, tok_scales, w0, w1, w2, w3, g
             scales = keep.tile([P, width], U8, name=name + "_scales", align_bytes=64)
             return codes, scales
 
-        def quantise(codes, scales, grouped, cols):
-            nc.vector.quantize_mx(out=codes[:, cols].bitcast(FP8X4), scales=scales[:, cols], in_=grouped[:, cols, :].rearrange("p c r -> p (c r)"))
+        def quantise(codes, scales, values):
+            nc.vector.quantize_mx(out=codes.bitcast(FP8X4), scales=scales, in_=values)
 
-        def gather(name, window, dtype, place, tag, first=0, count=J):
-            picked = keep.tile([P, count], dtype, name=name, tag=tag, align_bytes=64)
-            nc.vector.tensor_copy(out=picked[:], in_=window[:].indirect(offsets[place][:, first // 16 : (first + count) // 16]))
+        def gather(name, window, dtype, place, tag):
+            picked = keep.tile([P, J], dtype, name=name, tag=tag, align_bytes=64)
+            nc.vector.tensor_copy(out=picked[:], in_=window[:].indirect(offsets[place][:]))
             return picked
 
         halves = (slice(0, F // 2), slice(F // 2, F))
-        whole = slice(0, F)
 
-        nc.vector.memset(pool_scales[:].bitcast(I32), 0)
+        nc.gpsimd.memset(pool_scales[:].bitcast(I32), 0)
         nc.sync.dma_start(offsets[0][:], lists[0])
+
         nc.sync.dma_start(out=pool_words[:].bitcast(I32), in_=tok_words[0].bitcast(I32))
-        for q in range(4):
+        for r in range(4):
             nc.sync.dma_start(
-                out=pool_scales[32 * q : 32 * q + 4, :].bitcast(I32),
-                in_=tok_scales[0, 4 * q : 4 * q + 4, :].bitcast(I32),
+                out=pool_scales[r:P:32, :].bitcast(I32),
+                in_=tok_scales[0, r:16:4, :].bitcast(I32),
             )
         nc.sync.dma_start(offsets[1][:], lists[1])
         raw = {}
@@ -84,83 +91,104 @@ def tile_attend_nsa_compress_kernel(tc, tok_words, tok_scales, w0, w1, w2, w3, g
         nc.vector.memset(warm[:, 0:1], 0.0)
         warm_out = keep.tile([P, 1], F32, name="warm_out")
         nc.scalar.activation(out=warm_out[:], in_=warm[:, 0:1], func=GELU)
-        identity = keep.tile([P, P], F32, name="identity")
-        make_identity(nc, identity[:])
 
-        grouped = [keep.tile([P, F, PACK], BF16, name="grouped%d" % i, tag="grouped%d" % i, align_bytes=64) for i in range(PLACES)]
+        grouped = [keep.tile([P, PACK, P, PACK], BF16, name="grouped%d" % i, align_bytes=64) for i in range(PLACES)]
         wq = [planes("w%d" % i, F) for i in range(PLACES)]
-        z = [psum.tile([P, F], F32, name="z%d" % b) for b in range(J // P)]
+        z = [psum.tile([P, J], F32, name="z%d" % t, tag="z%d" % t) for t in range(PACK)]
 
-        def multiply(place, words, scales, blocks):
-            for n, b in enumerate(blocks):
-                cols = slice(n * P, (n + 1) * P)
-                nc.tensor.matmul_mx(
-                    out=z[b][:],
-                    lhsT=words[:, cols].bitcast(FP4X4),
-                    lhsT_scale=scales[:, cols],
-                    rhs=wq[place][0][:].bitcast(FP8X4),
-                    rhs_scale=wq[place][1][:],
-                    start=(place == 0),
-                    stop=(place == PLACES - 1),
-                )
+        def multiply(place, words, scales, t):
+            cols = slice(t * P, (t + 1) * P)
+            nc.tensor.matmul_mx(
+                out=z[t][:],
+                lhsT=wq[place][0][:, cols].bitcast(FP8X4),
+                lhsT_scale=wq[place][1][:, cols],
+                rhs=words[:].bitcast(FP4X4),
+                rhs_scale=scales[:],
+                start=(place == 0),
+                stop=(place == PLACES - 1),
+            )
 
-        def both_halves(place):
-            for u in range(2):
-                cast(raw[place, u], grouped[place], halves[u])
-            quantise(*wq[place], grouped[place], whole)
+        def prepare(place):
+            cast_dealt(raw[place, 0][:], grouped[place], 0, nc.scalar.copy)
+            if place == PLACES - 1:
+                cast_dealt(raw[place, 1][:, :, 0:SPLIT], grouped[place], P // 2, nc.scalar.copy)
+                cast_dealt(raw[place, 1][:, :, SPLIT : F // 2], grouped[place], P // 2 + SPLIT // PACK, nc.vector.tensor_copy)
+            else:
+                cast_dealt(raw[place, 1][:], grouped[place], P // 2, nc.scalar.copy)
+                quantise(wq[place][0][:], wq[place][1][:], grouped[place][:].rearrange("p t m r -> p (t m r)"))
 
         words0 = gather("words0", pool_words, U16, 0, "words0")
-        words1 = gather("words1", pool_words, U16, 1, "words1")
         scales0 = gather("scales0", pool_scales, U8, 0, "scales0")
-        both_halves(0)
-        multiply(0, words0, scales0, range(4))
-        scales1 = gather("scales1", pool_scales, U8, 1, "raw01")
-        both_halves(1)
-        multiply(1, words1, scales1, range(4))
-        words2 = gather("words2", pool_words, U16, 2, "raw10")
-        scales2 = gather("scales2", pool_scales, U8, 2, "raw11")
-        both_halves(2)
-        multiply(2, words2, scales2, range(4))
-        words3a = gather("words3a", pool_words, U16, 3, "raw21", 0, J // 2)
-        cast(raw[3, 0], grouped[3], halves[0])
-        quantise(*wq[3], grouped[3], halves[0])
-        scales3a = gather("scales3a", pool_scales, U8, 3, "raw30", 0, J // 2)
-        cast(raw[3, 1], grouped[3], halves[1])
-        quantise(*wq[3], grouped[3], halves[1])
-        multiply(3, words3a, scales3a, (0, 1))
-        words3b = gather("words3b", pool_words, U16, 3, "raw31", J // 2, J // 2)
-        scales3b = gather("scales3b", pool_scales, U8, 3, "grouped3", J // 2, J // 2)
-        grouped_wo = keep.tile([P, D, PACK], BF16, name="grouped_wo", align_bytes=64)
-        cast(raw_wo, grouped_wo, slice(0, D))
+        words1 = gather("words1", pool_words, U16, 1, "words1")
+        scales1 = gather("scales1", pool_scales, U8, 1, "scales1")
+        prepare(0)
+        for t in range(PACK):
+            multiply(0, words0, scales0, t)
+        words2 = gather("words2", pool_words, U16, 2, "raw01")
+        scales2 = gather("scales2", pool_scales, U8, 2, "raw10")
+        prepare(1)
+        for t in range(PACK):
+            multiply(1, words1, scales1, t)
+        words3 = gather("words3", pool_words, U16, 3, "raw11")
+        prepare(2)
+        for t in range(PACK):
+            multiply(2, words2, scales2, t)
+        scales3 = gather("scales3", pool_scales, U8, 3, "raw21")
+        prepare(3)
+        for t in range(PACK):
+            cols = slice(t * P, (t + 1) * P)
+            quantise(wq[3][0][:, cols], wq[3][1][:, cols], grouped[3][:, t, :, :].rearrange("p m r -> p (m r)"))
+            multiply(3, words3, scales3, t)
+        grouped_wo = keep.tile([P, D, PACK], BF16, name="grouped_wo", tag="raw31", align_bytes=64)
+        cast(raw_wo[:, :, 0 : D // 2], grouped_wo[:, 0 : D // 2, :], nc.scalar.copy)
+        cast(raw_wo[:, :, D // 2 : D], grouped_wo[:, D // 2 : D, :], nc.vector.tensor_copy)
         wo_codes, wo_scales = planes("wo", D)
-        quantise(wo_codes, wo_scales, grouped_wo, slice(0, D))
+        quantise(wo_codes[:], wo_scales[:], grouped_wo[:].rearrange("p c r -> p (c r)"))
 
-        out_rows = out.rearrange("(h p) j -> p h j", p=P)
-        for b in range(J // P):
-            if b == 1:
-                multiply(3, words3b, scales3b, (2, 3))
-            act = keep.tile([P, PACK, P], F32, name="act%d" % b)
-            dealt = z[b][:].rearrange("p (m t) -> p t m", t=PACK)
-            step = 2 if b == 0 else PACK
-            for t in range(0, PACK, step):
-                nc.scalar.activation(out=act[:, t : t + step, :], in_=dealt[:, t : t + step, :], func=GELU)
-            turned = psum.tile([P, PACK, P], F32, name="turned%d" % b, tag="turned", bufs=2)
-            for t in range(PACK):
-                nc.tensor.transpose(turned[:, t, :], act[:, t, :], identity[:])
-            g = keep.tile([P, P, PACK], BF16, name="g%d" % b, align_bytes=64)
-            nc.vector.tensor_tensor(
-                out=g[:],
-                in0=turned[:].rearrange("p t j -> p j t"),
-                in1=gains[:].unsqueeze(1).to_broadcast([P, P, PACK]),
-                op=MULT,
+        H = J // 2
+        act = [keep.tile([P, J], F32, name="act%d" % t) for t in range(PACK)]
+        pairs = [keep.tile([P, 2, H, 2], BF16, name="pairs%d" % h, align_bytes=64) for h in range(2)]
+        def scale_by_gain(t, h):
+            cols = slice(h * H, (h + 1) * H)
+            nc.vector.tensor_scalar(out=pairs[h][:, t // 2, :, t % 2], in0=act[t][:, cols], scalar1=gains[:, t : t + 1], scalar2=None, op0=MULT)
+
+        def keep_warm(t):
+            spare = psum.tile([P, J], F32, name="spare%d" % t, tag="z%d" % t)
+            nc.tensor.matmul_mx(
+                out=spare[:],
+                lhsT=wq[3][0][:, 0:P].bitcast(FP8X4),
+                lhsT_scale=wq[3][1][:, 0:P],
+                rhs=words3[:].bitcast(FP4X4),
+                rhs_scale=scales3[:],
+                start=True,
+                stop=True,
             )
-            g_codes, g_scales = planes("g%d" % b, P)
-            quantise(g_codes, g_scales, g, slice(0, P))
-            y = psum.tile([P, D // P, P], F32, name="y%d" % b, tag="y", bufs=2)
-            for h in range(D // P):
-                cols = slice(h * P, (h + 1) * P)
+
+        for t in range(2):
+            nc.scalar.activation(out=act[t][:], in_=z[t][:], func=GELU)
+            keep_warm(t)
+            for h in range(2):
+                scale_by_gain(t, h)
+        for h in range(2):
+            for t in range(2, PACK):
+                cols = slice(h * H, (h + 1) * H)
+                nc.scalar.activation(out=act[t][:, cols], in_=z[t][:, cols], func=GELU)
+                scale_by_gain(t, h)
+        keep_warm(2)
+        keep_warm(3)
+        for h, copy in enumerate((nc.scalar.copy, nc.vector.tensor_copy)):
+            g = keep.tile([P, H * PACK], BF16, name="g%d" % h, align_bytes=64)
+            copy(
+                out=g[:].bitcast(F32).rearrange("p (c i u) -> p c u i", i=4, u=2),
+                in_=pairs[h][:].rearrange("p u j e -> p (u j e)").bitcast(F32).rearrange("p (u c i) -> p c u i", u=2, i=4),
+            )
+            g_codes, g_scales = planes("g%d" % h, H)
+            quantise(g_codes[:], g_scales[:], g[:])
+            for d, evict in enumerate((nc.scalar.copy, nc.vector.tensor_copy)):
+                cols = slice(d * P, (d + 1) * P)
+                y = psum.tile([P, H], F32, name="y%d%d" % (h, d))
                 nc.tensor.matmul_mx(
-                    out=y[:, h, :],
+                    out=y[:],
                     lhsT=wo_codes[:, cols].bitcast(FP8X4),
                     lhsT_scale=wo_scales[:, cols],
                     rhs=g_codes[:].bitcast(FP8X4),
@@ -168,6 +196,6 @@ def tile_attend_nsa_compress_kernel(tc, tok_words, tok_scales, w0, w1, w2, w3, g
                     start=True,
                     stop=True,
                 )
-            result = keep.tile([P, D // P, P], F32, name="result%d" % b)
-            nc.scalar.copy(out=result[:], in_=y[:])
-            nc.sync.dma_start(out=out_rows[:, :, b * P : (b + 1) * P], in_=result[:])
+                result = keep.tile([P, H], F32, name="result%d%d" % (h, d))
+                evict(out=result[:], in_=y[:])
+                nc.sync.dma_start(out=out[cols, h * H : (h + 1) * H], in_=result[:])

@@ -111,8 +111,7 @@ def tile_attend_nsa_compress_kernel(tc, tok_words, tok_scales, w0, w1, w2, w3, g
         def prepare(place):
             cast_dealt(raw[place, 0][:], grouped[place], 0, nc.scalar.copy)
             if place == PLACES - 1:
-                cast_dealt(raw[place, 1][:, :, 0:SPLIT], grouped[place], P // 2, nc.scalar.copy)
-                cast_dealt(raw[place, 1][:, :, SPLIT : F // 2], grouped[place], P // 2 + SPLIT // PACK, nc.vector.tensor_copy)
+                cast_dealt(raw[place, 1][:], grouped[place], P // 2, nc.vector.tensor_copy)
             else:
                 cast_dealt(raw[place, 1][:], grouped[place], P // 2, nc.scalar.copy)
                 quantise(wq[place][0][:], wq[place][1][:], grouped[place][:].rearrange("p t m r -> p (t m r)"))
@@ -139,18 +138,19 @@ def tile_attend_nsa_compress_kernel(tc, tok_words, tok_scales, w0, w1, w2, w3, g
             cols = slice(t * P, (t + 1) * P)
             quantise(wq[3][0][:, cols], wq[3][1][:, cols], grouped[3][:, t, :, :].rearrange("p m r -> p (m r)"))
             multiply(3, words3, scales3, t)
-        grouped_wo = keep.tile([P, D, PACK], BF16, name="grouped_wo", tag="raw31", align_bytes=64)
-        cast(raw_wo[:, :, 0 : D // 2], grouped_wo[:, 0 : D // 2, :], nc.scalar.copy)
-        cast(raw_wo[:, :, D // 2 : D], grouped_wo[:, D // 2 : D, :], nc.vector.tensor_copy)
+        grouped_wo = keep.tile([P, D, PACK], BF16, name="grouped_wo", align_bytes=64)
+        cast(raw_wo[:], grouped_wo[:], nc.scalar.copy)
         wo_codes, wo_scales = planes("wo", D)
         quantise(wo_codes[:], wo_scales[:], grouped_wo[:].rearrange("p c r -> p (c r)"))
 
         H = J // 2
         act = [keep.tile([P, J], F32, name="act%d" % t) for t in range(PACK)]
-        pairs = [keep.tile([P, 2, H, 2], BF16, name="pairs%d" % h, align_bytes=64) for h in range(2)]
-        def scale_by_gain(t, h):
-            cols = slice(h * H, (h + 1) * H)
-            nc.vector.tensor_scalar(out=pairs[h][:, t // 2, :, t % 2], in0=act[t][:, cols], scalar1=gains[:, t : t + 1], scalar2=None, op0=MULT)
+        pairs = keep.tile([P, J * PACK], BF16, name="pairs", tag="pairs", align_bytes=64)
+        pair_view = pairs[:].rearrange("p (h u j e) -> p h u j e", h=2, u=2, e=2)
+
+        def scale_by_gain(t, hs):
+            values = act[t][:].rearrange("p (h j) -> p h j", h=2)[:, hs, :]
+            nc.vector.tensor_scalar(out=pair_view[:, hs, t // 2, :, t % 2], in0=values, scalar1=gains[:, t : t + 1], scalar2=None, op0=MULT)
 
         def keep_warm(t):
             spare = psum.tile([P, J], F32, name="spare%d" % t, tag="z%d" % t)
@@ -167,23 +167,24 @@ def tile_attend_nsa_compress_kernel(tc, tok_words, tok_scales, w0, w1, w2, w3, g
         for t in range(2):
             nc.scalar.activation(out=act[t][:], in_=z[t][:], func=GELU)
             keep_warm(t)
-            for h in range(2):
-                scale_by_gain(t, h)
+            scale_by_gain(t, slice(0, 2))
         for h in range(2):
             for t in range(2, PACK):
                 cols = slice(h * H, (h + 1) * H)
                 nc.scalar.activation(out=act[t][:, cols], in_=z[t][:, cols], func=GELU)
-                scale_by_gain(t, h)
+                scale_by_gain(t, slice(h, h + 1))
         keep_warm(2)
         keep_warm(3)
+        gq = []
         for h, copy in enumerate((nc.scalar.copy, nc.vector.tensor_copy)):
-            g = keep.tile([P, H * PACK], BF16, name="g%d" % h, align_bytes=64)
+            g = keep.tile([P, H * PACK], BF16, name="g%d" % h, tag="g%d" % h, align_bytes=64)
             copy(
                 out=g[:].bitcast(F32).rearrange("p (c i u) -> p c u i", i=4, u=2),
-                in_=pairs[h][:].rearrange("p u j e -> p (u j e)").bitcast(F32).rearrange("p (u c i) -> p c u i", u=2, i=4),
+                in_=pairs[:, h * H * PACK : (h + 1) * H * PACK].bitcast(F32).rearrange("p (u c i) -> p c u i", u=2, i=4),
             )
-            g_codes, g_scales = planes("g%d" % h, H)
-            quantise(g_codes[:], g_scales[:], g[:])
+            gq.append(planes("g%d" % h, H))
+            quantise(gq[h][0][:], gq[h][1][:], g[:])
+        for h in range(2):
             for d, evict in enumerate((nc.scalar.copy, nc.vector.tensor_copy)):
                 cols = slice(d * P, (d + 1) * P)
                 y = psum.tile([P, H], F32, name="y%d%d" % (h, d))
@@ -191,11 +192,11 @@ def tile_attend_nsa_compress_kernel(tc, tok_words, tok_scales, w0, w1, w2, w3, g
                     out=y[:],
                     lhsT=wo_codes[:, cols].bitcast(FP8X4),
                     lhsT_scale=wo_scales[:, cols],
-                    rhs=g_codes[:].bitcast(FP8X4),
-                    rhs_scale=g_scales[:],
+                    rhs=gq[h][0][:].bitcast(FP8X4),
+                    rhs_scale=gq[h][1][:],
                     start=True,
                     stop=True,
                 )
-                result = keep.tile([P, H], F32, name="result%d%d" % (h, d))
+                result = keep.tile([P, H], F32, name="result%d%d" % (h, d), tag="g1" if (h, d) == (0, 1) else "result%d%d" % (h, d), align_bytes=64)
                 evict(out=result[:], in_=y[:])
                 nc.sync.dma_start(out=out[cols, h * H : (h + 1) * H], in_=result[:])

@@ -6,7 +6,11 @@ K, T, J, F, D = 512, 2048, 512, 512, 256
 P = 128
 PACK = 4
 PLACES = 4
-SPLIT = 128
+LIST_ROWS = 16
+SCALE_ROWS = 16
+QUADRANT = 32
+RUN = 4
+H = J // 2
 FLOPS = 2 * PLACES * K * F * J + 2 * F * D * J
 
 F32 = mybir.dt.float32
@@ -20,39 +24,26 @@ FP4X4 = mybir.dt.float4_e2m1fn_x4
 GELU = mybir.ActivationFunctionType.Gelu_apprx_tanh
 MULT = mybir.AluOpType.mult
 
+HALVES = (slice(0, F // 2), slice(F // 2, F))
+LAST_PIECES = (slice(0, F // 2), slice(F // 2, 3 * F // 4), slice(3 * F // 4, F))
+PIECES = (HALVES, HALVES, HALVES, LAST_PIECES)
+
 
 def tile_attend_nsa_compress_kernel(tc, tok_words, tok_scales, w0, w1, w2, w3, gain, wo, offs, offs2, offs3, offs4, out):
     nc = tc.nc
     weights = (w0, w1, w2, w3)
     lists = (offs, offs2, offs3, offs4)
+    last = PLACES - 1
     with ExitStack() as ctx:
         keep = ctx.enter_context(tc.tile_pool(name="keep", bufs=1))
         psum = ctx.enter_context(tc.psum_pool(name="psum", bufs=1))
 
-        pool_words = keep.tile([P, T], U16, name="pool_words", align_bytes=64)
-        pool_scales = keep.tile([P, T], U8, name="pool_scales", align_bytes=64)
-        offsets = [keep.tile([P, J // 16], U16, name="offsets%d" % i) for i in range(PLACES)]
-
-        def load_columns(name, w, cols):
-            width = cols.stop - cols.start
-            raw = keep.tile([P, PACK, width], F32, name=name, tag=name, align_bytes=64)
-            nc.sync.dma_start(out=raw[:], in_=w.rearrange("(p r) c -> p r c", r=PACK)[:, :, cols])
+        def load_columns(name, matrix, cols):
+            raw = keep.tile([P, PACK, cols.stop - cols.start], F32, name=name, tag=name, align_bytes=64)
+            nc.sync.dma_start(out=raw[:], in_=matrix.rearrange("(p r) c -> p r c", r=PACK)[:, :, cols])
             return raw
 
-        def cast(raw, grouped, copy):
-            copy(
-                out=grouped.rearrange("p (c i) r -> p c r i", i=4),
-                in_=raw.rearrange("p r (c i) -> p c r i", i=4),
-            )
-
-        def cast_dealt(raw, grouped, first, copy):
-            m = slice(first, first + raw.shape[2] // PACK)
-            copy(
-                out=grouped[:, :, m, :].rearrange("p t m r -> p m r t"),
-                in_=raw.rearrange("p r (m t) -> p m r t", t=PACK),
-            )
-
-        def planes(name, width):
+        def mx_tiles(name, width):
             codes = keep.tile([P, width], U32, name=name + "_codes", align_bytes=64)
             scales = keep.tile([P, width], U8, name=name + "_scales", align_bytes=64)
             return codes, scales
@@ -60,104 +51,117 @@ def tile_attend_nsa_compress_kernel(tc, tok_words, tok_scales, w0, w1, w2, w3, g
         def quantise(codes, scales, values):
             nc.vector.quantize_mx(out=codes.bitcast(FP8X4), scales=scales, in_=values)
 
+        pool_words = keep.tile([P, T], U16, name="pool_words", align_bytes=64)
+        pool_scales = keep.tile([P, T], U8, name="pool_scales", align_bytes=64)
+        offsets = [keep.tile([P, J // LIST_ROWS], U16, name="offsets%d" % place) for place in range(PLACES)]
+        rows_in_quadrant = SCALE_ROWS * QUADRANT // P
+        nc.gpsimd.memset(pool_scales[:].bitcast(I32), 0)
+        nc.sync.dma_start(offsets[0][:], lists[0])
+        nc.sync.dma_start(out=pool_words[:].bitcast(I32), in_=tok_words[0].bitcast(I32))
+        for r in range(rows_in_quadrant):
+            nc.sync.dma_start(
+                out=pool_scales[r:P:QUADRANT, :].bitcast(I32),
+                in_=tok_scales[0, r:SCALE_ROWS:rows_in_quadrant, :].bitcast(I32),
+            )
+        nc.sync.dma_start(offsets[1][:], lists[1])
+        raw = {}
+        for place in range(PLACES):
+            for n, cols in enumerate(PIECES[place]):
+                raw[place, n] = load_columns("raw%d%d" % (place, n), weights[place], cols)
+                if place == 1:
+                    nc.sync.dma_start(offsets[2 + n][:], lists[2 + n])
+        raw_wo = load_columns("raw_wo", wo, slice(0, D))
+        gains = keep.tile([P, PACK], F32, name="gains")
+        nc.sync.dma_start(out=gains[:], in_=gain.rearrange("(p t) o -> p (t o)", t=PACK))
+
+        warm_in = keep.tile([P, 1], F32, name="warm_in")
+        nc.vector.memset(warm_in[:], 0.0)
+        warm_out = keep.tile([P, 1], F32, name="warm_out")
+        nc.scalar.activation(out=warm_out[:], in_=warm_in[:], func=GELU)
+
+        dealt = [keep.tile([P, PACK, P, PACK], BF16, name="dealt%d" % place, align_bytes=64) for place in range(PLACES)]
+        w_mx = [mx_tiles("w%d" % place, F) for place in range(PLACES)]
+        z = [psum.tile([P, J], F32, name="z%d" % t, tag="z%d" % t) for t in range(PACK)]
+
         def gather(name, window, dtype, place, tag):
             picked = keep.tile([P, J], dtype, name=name, tag=tag, align_bytes=64)
             nc.vector.tensor_copy(out=picked[:], in_=window[:].indirect(offsets[place][:]))
             return picked
 
-        halves = (slice(0, F // 2), slice(F // 2, F))
+        def cast_weights(place):
+            for n, cols in enumerate(PIECES[place]):
+                m = slice(cols.start // PACK, cols.stop // PACK)
+                nc.scalar.copy(
+                    out=dealt[place][:, :, m, :].rearrange("p t m r -> p m r t"),
+                    in_=raw[place, n][:].rearrange("p r (m t) -> p m r t", t=PACK),
+                )
 
-        nc.gpsimd.memset(pool_scales[:].bitcast(I32), 0)
-        nc.sync.dma_start(offsets[0][:], lists[0])
-
-        nc.sync.dma_start(out=pool_words[:].bitcast(I32), in_=tok_words[0].bitcast(I32))
-        for r in range(4):
-            nc.sync.dma_start(
-                out=pool_scales[r:P:32, :].bitcast(I32),
-                in_=tok_scales[0, r:16:4, :].bitcast(I32),
-            )
-        nc.sync.dma_start(offsets[1][:], lists[1])
-        raw = {}
-        for i in range(PLACES):
-            for u in range(2):
-                raw[i, u] = load_columns("raw%d%d" % (i, u), weights[i], halves[u])
-                if i == 1:
-                    nc.sync.dma_start(offsets[2 + u][:], lists[2 + u])
-        raw_wo = load_columns("raw_wo", wo, slice(0, D))
-        gains = keep.tile([P, PACK], F32, name="gains")
-        nc.sync.dma_start(out=gains[:], in_=gain.rearrange("(p r) o -> p (r o)", r=PACK))
-
-        warm = keep.tile([P, 2], F32, name="warm")
-        nc.vector.memset(warm[:, 0:1], 0.0)
-        warm_out = keep.tile([P, 1], F32, name="warm_out")
-        nc.scalar.activation(out=warm_out[:], in_=warm[:, 0:1], func=GELU)
-
-        grouped = [keep.tile([P, PACK, P, PACK], BF16, name="grouped%d" % i, align_bytes=64) for i in range(PLACES)]
-        wq = [planes("w%d" % i, F) for i in range(PLACES)]
-        z = [psum.tile([P, J], F32, name="z%d" % t, tag="z%d" % t) for t in range(PACK)]
+        def quantise_weights(place):
+            quantise(w_mx[place][0][:], w_mx[place][1][:], dealt[place][:].rearrange("p t m r -> p (t m r)"))
 
         def multiply(place, words, scales, t):
             cols = slice(t * P, (t + 1) * P)
             nc.tensor.matmul_mx(
                 out=z[t][:],
-                lhsT=wq[place][0][:, cols].bitcast(FP8X4),
-                lhsT_scale=wq[place][1][:, cols],
+                lhsT=w_mx[place][0][:, cols].bitcast(FP8X4),
+                lhsT_scale=w_mx[place][1][:, cols],
                 rhs=words[:].bitcast(FP4X4),
                 rhs_scale=scales[:],
                 start=(place == 0),
-                stop=(place == PLACES - 1),
+                stop=(place == last),
             )
-
-        def prepare(place):
-            cast_dealt(raw[place, 0][:], grouped[place], 0, nc.scalar.copy)
-            if place == PLACES - 1:
-                cast_dealt(raw[place, 1][:], grouped[place], P // 2, nc.vector.tensor_copy)
-            else:
-                cast_dealt(raw[place, 1][:], grouped[place], P // 2, nc.scalar.copy)
-                quantise(wq[place][0][:], wq[place][1][:], grouped[place][:].rearrange("p t m r -> p (t m r)"))
 
         words0 = gather("words0", pool_words, U16, 0, "words0")
         scales0 = gather("scales0", pool_scales, U8, 0, "scales0")
         words1 = gather("words1", pool_words, U16, 1, "words1")
         scales1 = gather("scales1", pool_scales, U8, 1, "scales1")
-        prepare(0)
+        cast_weights(0)
+        quantise_weights(0)
         for t in range(PACK):
             multiply(0, words0, scales0, t)
         words2 = gather("words2", pool_words, U16, 2, "raw01")
         scales2 = gather("scales2", pool_scales, U8, 2, "raw10")
-        prepare(1)
+        cast_weights(1)
+        quantise_weights(1)
         for t in range(PACK):
             multiply(1, words1, scales1, t)
         words3 = gather("words3", pool_words, U16, 3, "raw11")
-        prepare(2)
+        cast_weights(2)
+        quantise_weights(2)
         for t in range(PACK):
             multiply(2, words2, scales2, t)
         scales3 = gather("scales3", pool_scales, U8, 3, "raw21")
-        prepare(3)
+        cast_weights(last)
         for t in range(PACK):
             cols = slice(t * P, (t + 1) * P)
-            quantise(wq[3][0][:, cols], wq[3][1][:, cols], grouped[3][:, t, :, :].rearrange("p m r -> p (m r)"))
-            multiply(3, words3, scales3, t)
-        grouped_wo = keep.tile([P, D, PACK], BF16, name="grouped_wo", align_bytes=64)
-        cast(raw_wo[:], grouped_wo[:], nc.scalar.copy)
-        wo_codes, wo_scales = planes("wo", D)
-        quantise(wo_codes[:], wo_scales[:], grouped_wo[:].rearrange("p c r -> p (c r)"))
+            quantise(w_mx[last][0][:, cols], w_mx[last][1][:, cols], dealt[last][:, t, :, :].rearrange("p m r -> p (m r)"))
+            multiply(last, words3, scales3, t)
 
-        H = J // 2
+        grouped_wo = keep.tile([P, D, PACK], BF16, name="grouped_wo", tag="raw32", align_bytes=64)
+        for cols, copy in ((slice(0, D // 2), nc.scalar.copy), (slice(D // 2, D), nc.vector.tensor_copy)):
+            copy(
+                out=grouped_wo[:, cols, :].rearrange("p (c i) r -> p c r i", i=RUN),
+                in_=raw_wo[:, :, cols].rearrange("p r (c i) -> p c r i", i=RUN),
+            )
+        wo_codes, wo_scales = mx_tiles("wo", D)
+        quantise(wo_codes[:], wo_scales[:], grouped_wo[:].rearrange("p d r -> p (d r)"))
+
         act = [keep.tile([P, J], F32, name="act%d" % t) for t in range(PACK)]
-        pairs = keep.tile([P, J * PACK], BF16, name="pairs", tag="pairs", align_bytes=64)
+        pairs = keep.tile([P, J * PACK], BF16, name="pairs", align_bytes=64)
         pair_view = pairs[:].rearrange("p (h u j e) -> p h u j e", h=2, u=2, e=2)
 
-        def scale_by_gain(t, hs):
-            values = act[t][:].rearrange("p (h j) -> p h j", h=2)[:, hs, :]
-            nc.vector.tensor_scalar(out=pair_view[:, hs, t // 2, :, t % 2], in0=values, scalar1=gains[:, t : t + 1], scalar2=None, op0=MULT)
+        def scale_by_gain(t, halves):
+            values = act[t][:].rearrange("p (h j) -> p h j", h=2)[:, halves, :]
+            nc.vector.tensor_scalar(
+                out=pair_view[:, halves, t // 2, :, t % 2], in0=values, scalar1=gains[:, t : t + 1], scalar2=None, op0=MULT
+            )
 
-        def keep_warm(t):
+        def keep_tensor_busy(t):
             spare = psum.tile([P, J], F32, name="spare%d" % t, tag="z%d" % t)
             nc.tensor.matmul_mx(
                 out=spare[:],
-                lhsT=wq[3][0][:, 0:P].bitcast(FP8X4),
-                lhsT_scale=wq[3][1][:, 0:P],
+                lhsT=w_mx[last][0][:, 0:P].bitcast(FP8X4),
+                lhsT_scale=w_mx[last][1][:, 0:P],
                 rhs=words3[:].bitcast(FP4X4),
                 rhs_scale=scales3[:],
                 start=True,
@@ -166,37 +170,40 @@ def tile_attend_nsa_compress_kernel(tc, tok_words, tok_scales, w0, w1, w2, w3, g
 
         for t in range(2):
             nc.scalar.activation(out=act[t][:], in_=z[t][:], func=GELU)
-            keep_warm(t)
+            keep_tensor_busy(t)
             scale_by_gain(t, slice(0, 2))
         for h in range(2):
             for t in range(2, PACK):
                 cols = slice(h * H, (h + 1) * H)
                 nc.scalar.activation(out=act[t][:, cols], in_=z[t][:, cols], func=GELU)
                 scale_by_gain(t, slice(h, h + 1))
-        keep_warm(2)
-        keep_warm(3)
-        gq = []
+        for t in range(2, PACK):
+            keep_tensor_busy(t)
+
+        g_mx = []
         for h, copy in enumerate((nc.scalar.copy, nc.vector.tensor_copy)):
             g = keep.tile([P, H * PACK], BF16, name="g%d" % h, tag="g%d" % h, align_bytes=64)
             copy(
-                out=g[:].bitcast(F32).rearrange("p (c i u) -> p c u i", i=4, u=2),
-                in_=pairs[:, h * H * PACK : (h + 1) * H * PACK].bitcast(F32).rearrange("p (u c i) -> p c u i", u=2, i=4),
+                out=g[:].bitcast(F32).rearrange("p (c i u) -> p c u i", i=RUN, u=2),
+                in_=pairs[:, h * H * PACK : (h + 1) * H * PACK].bitcast(F32).rearrange("p (u c i) -> p c u i", u=2, i=RUN),
             )
-            gq.append(planes("g%d" % h, H))
-            quantise(gq[h][0][:], gq[h][1][:], g[:])
+            g_mx.append(mx_tiles("g%d" % h, H))
+            quantise(g_mx[h][0][:], g_mx[h][1][:], g[:])
+
         for h in range(2):
-            for d, evict in enumerate((nc.scalar.copy, nc.vector.tensor_copy)):
-                cols = slice(d * P, (d + 1) * P)
-                y = psum.tile([P, H], F32, name="y%d%d" % (h, d))
+            for block, copy in enumerate((nc.scalar.copy, nc.vector.tensor_copy)):
+                rows = slice(block * P, (block + 1) * P)
+                y = psum.tile([P, H], F32, name="y%d%d" % (h, block))
                 nc.tensor.matmul_mx(
                     out=y[:],
-                    lhsT=wo_codes[:, cols].bitcast(FP8X4),
-                    lhsT_scale=wo_scales[:, cols],
-                    rhs=gq[h][0][:].bitcast(FP8X4),
-                    rhs_scale=gq[h][1][:],
+                    lhsT=wo_codes[:, rows].bitcast(FP8X4),
+                    lhsT_scale=wo_scales[:, rows],
+                    rhs=g_mx[h][0][:].bitcast(FP8X4),
+                    rhs_scale=g_mx[h][1][:],
                     start=True,
                     stop=True,
                 )
-                result = keep.tile([P, H], F32, name="result%d%d" % (h, d), tag="g1" if (h, d) == (0, 1) else "result%d%d" % (h, d), align_bytes=64)
-                evict(out=result[:], in_=y[:])
-                nc.sync.dma_start(out=out[cols, h * H : (h + 1) * H], in_=result[:])
+                name = "result%d%d" % (h, block)
+                result = keep.tile([P, H], F32, name=name, tag="g1" if (h, block) == (0, 1) else name, align_bytes=64)
+                copy(out=result[:], in_=y[:])
+                nc.sync.dma_start(out=out[rows, h * H : (h + 1) * H], in_=result[:])

@@ -10,6 +10,8 @@ LIST_ROWS = 16
 SCALE_ROWS = 16
 QUADRANT = 32
 RUN = 4
+QUARTERS = 4
+Q = J // QUARTERS
 H = J // 2
 FLOPS = 2 * PLACES * K * F * J + 2 * F * D * J
 
@@ -24,9 +26,10 @@ FP4X4 = mybir.dt.float4_e2m1fn_x4
 GELU = mybir.ActivationFunctionType.Gelu_apprx_tanh
 MULT = mybir.AluOpType.mult
 
+SLOT = PACK * (F // 2) * 4
 HALVES = (slice(0, F // 2), slice(F // 2, F))
-LAST_PIECES = (slice(0, F // 2), slice(F // 2, 3 * F // 4), slice(3 * F // 4, F))
-PIECES = (HALVES, HALVES, HALVES, LAST_PIECES)
+FIRST_PIECES = (slice(0, F // 4), slice(F // 4, F))
+W_PIECES = (FIRST_PIECES, HALVES, HALVES, HALVES)
 
 
 def tile_attend_nsa_compress_kernel(tc, tok_words, tok_scales, w0, w1, w2, w3, gain, wo, offs, offs2, offs3, offs4, out):
@@ -38,8 +41,10 @@ def tile_attend_nsa_compress_kernel(tc, tok_words, tok_scales, w0, w1, w2, w3, g
         keep = ctx.enter_context(tc.tile_pool(name="keep", bufs=1))
         psum = ctx.enter_context(tc.psum_pool(name="psum", bufs=1))
 
-        def load_columns(name, matrix, cols):
-            raw = keep.tile([P, PACK, cols.stop - cols.start], F32, name=name, tag=name, align_bytes=64)
+        stage = ctx.enter_context(tc.tile_pool(name="stage", bufs=1))
+
+        def load_columns(name, matrix, cols, slot):
+            raw = stage.tile([P, PACK, cols.stop - cols.start], F32, name=name, align_bytes=64, offset=slot)
             nc.sync.dma_start(out=raw[:], in_=matrix.rearrange("(p r) c -> p r c", r=PACK)[:, :, cols])
             return raw
 
@@ -55,41 +60,54 @@ def tile_attend_nsa_compress_kernel(tc, tok_words, tok_scales, w0, w1, w2, w3, g
         pool_scales = keep.tile([P, T], U8, name="pool_scales", align_bytes=64)
         offsets = [keep.tile([P, J // LIST_ROWS], U16, name="offsets%d" % place) for place in range(PLACES)]
         rows_in_quadrant = SCALE_ROWS * QUADRANT // P
-        nc.gpsimd.memset(pool_scales[:].bitcast(I32), 0)
-        nc.sync.dma_start(offsets[0][:], lists[0])
-        nc.sync.dma_start(out=pool_words[:].bitcast(I32), in_=tok_words[0].bitcast(I32))
-        for r in range(rows_in_quadrant):
-            nc.sync.dma_start(
-                out=pool_scales[r:P:QUADRANT, :].bitcast(I32),
-                in_=tok_scales[0, r:SCALE_ROWS:rows_in_quadrant, :].bitcast(I32),
-            )
-        nc.sync.dma_start(offsets[1][:], lists[1])
-        raw = {}
-        for place in range(PLACES):
-            for n, cols in enumerate(PIECES[place]):
-                raw[place, n] = load_columns("raw%d%d" % (place, n), weights[place], cols)
-                if place == 1:
-                    nc.sync.dma_start(offsets[2 + n][:], lists[2 + n])
-        raw_wo = load_columns("raw_wo", wo, slice(0, D))
-        gains = keep.tile([P, PACK], F32, name="gains")
-        nc.sync.dma_start(out=gains[:], in_=gain.rearrange("(p t) o -> p (t o)", t=PACK))
-
+        nc.vector.memset(pool_scales[:, 0 : T // 2].bitcast(I32), 0)
+        nc.gpsimd.memset(pool_scales[:, T // 2 : T].bitcast(I32), 0)
+        for place in range(2):
+            nc.sync.dma_start(offsets[place][:], lists[place])
         warm_in = keep.tile([P, 1], F32, name="warm_in")
         nc.vector.memset(warm_in[:], 0.0)
         warm_out = keep.tile([P, 1], F32, name="warm_out")
         nc.scalar.activation(out=warm_out[:], in_=warm_in[:], func=GELU)
 
+        raw = {}
+
+        def load_half(place, n):
+            raw[place, n] = load_columns("raw%d%d" % (place, n), weights[place], W_PIECES[place][n], 2 * place * SLOT + PACK * 4 * W_PIECES[place][n].start)
+
+        load_half(0, 0)
+        for r in range(rows_in_quadrant):
+            nc.sync.dma_start(
+                out=pool_scales[r:P:QUADRANT, :].bitcast(I32),
+                in_=tok_scales[0, r:SCALE_ROWS:rows_in_quadrant, :].bitcast(I32),
+            )
+        load_half(0, 1)
+        nc.sync.dma_start(offsets[2][:], lists[2])
+        load_half(1, 0)
+        nc.sync.dma_start(offsets[3][:], lists[3])
+        nc.sync.dma_start(out=pool_words[:].bitcast(I32), in_=tok_words[0].bitcast(I32))
+        load_half(1, 1)
+        for place in (2, 3):
+            for n in range(2):
+                load_half(place, n)
+        raw_wo = load_columns("raw_wo", wo, slice(0, D), 2 * PLACES * SLOT)
+        gains = keep.tile([P, PACK], F32, name="gains")
+        nc.sync.dma_start(out=gains[:], in_=gain.rearrange("(p t) o -> p (t o)", t=PACK))
+
         dealt = [keep.tile([P, PACK, P, PACK], BF16, name="dealt%d" % place, align_bytes=64) for place in range(PLACES)]
         w_mx = [mx_tiles("w%d" % place, F) for place in range(PLACES)]
-        z = [psum.tile([P, J], F32, name="z%d" % t, tag="z%d" % t) for t in range(PACK)]
+        z = [psum.tile([P, PACK, Q], F32, name="z%d" % q) for q in range(QUARTERS)]
 
-        def gather(name, window, dtype, place, tag):
-            picked = keep.tile([P, J], dtype, name=name, tag=tag, align_bytes=64)
-            nc.vector.tensor_copy(out=picked[:], in_=window[:].indirect(offsets[place][:]))
+        def gather(name, window, dtype, place, at=None, first=0, count=J):
+            if at is None:
+                picked = keep.tile([P, count], dtype, name=name, align_bytes=64)
+            else:
+                picked = stage.tile([P, count], dtype, name=name, align_bytes=64, offset=at)
+            entries = offsets[place][:, first // LIST_ROWS : (first + count) // LIST_ROWS]
+            nc.vector.tensor_copy(out=picked[:], in_=window[:].indirect(entries))
             return picked
 
         def cast_weights(place):
-            for n, cols in enumerate(PIECES[place]):
+            for n, cols in enumerate(W_PIECES[place]):
                 m = slice(cols.start // PACK, cols.stop // PACK)
                 nc.scalar.copy(
                     out=dealt[place][:, :, m, :].rearrange("p t m r -> p m r t"),
@@ -99,111 +117,71 @@ def tile_attend_nsa_compress_kernel(tc, tok_words, tok_scales, w0, w1, w2, w3, g
         def quantise_weights(place):
             quantise(w_mx[place][0][:], w_mx[place][1][:], dealt[place][:].rearrange("p t m r -> p (t m r)"))
 
-        def multiply(place, words, scales, t):
-            cols = slice(t * P, (t + 1) * P)
-            nc.tensor.matmul_mx(
-                out=z[t][:],
-                lhsT=w_mx[place][0][:, cols].bitcast(FP8X4),
-                lhsT_scale=w_mx[place][1][:, cols],
-                rhs=words[:].bitcast(FP4X4),
-                rhs_scale=scales[:],
-                start=(place == 0),
-                stop=(place == last),
-            )
+        def multiply(place, q, words, scales, first):
+            for t in range(PACK):
+                cols = slice(t * P, (t + 1) * P)
+                blocks = slice(q * Q - first, (q + 1) * Q - first)
+                nc.tensor.matmul_mx(
+                    out=z[q][:, t, :],
+                    lhsT=w_mx[place][0][:, cols].bitcast(FP8X4),
+                    lhsT_scale=w_mx[place][1][:, cols],
+                    rhs=words[:, blocks].bitcast(FP4X4),
+                    rhs_scale=scales[:, blocks],
+                    start=(place == 0 and t == 0),
+                    stop=(place == last and t == PACK - 1),
+                )
 
-        words0 = gather("words0", pool_words, U16, 0, "words0")
-        scales0 = gather("scales0", pool_scales, U8, 0, "scales0")
-        words1 = gather("words1", pool_words, U16, 1, "words1")
-        scales1 = gather("scales1", pool_scales, U8, 1, "scales1")
-        cast_weights(0)
-        quantise_weights(0)
-        for t in range(PACK):
-            multiply(0, words0, scales0, t)
-        words2 = gather("words2", pool_words, U16, 2, "raw01")
-        scales2 = gather("scales2", pool_scales, U8, 2, "raw10")
-        cast_weights(1)
-        quantise_weights(1)
-        for t in range(PACK):
-            multiply(1, words1, scales1, t)
-        words3 = gather("words3", pool_words, U16, 3, "raw11")
-        cast_weights(2)
-        quantise_weights(2)
-        for t in range(PACK):
-            multiply(2, words2, scales2, t)
-        scales3 = gather("scales3", pool_scales, U8, 3, "raw21")
+        scales = [gather("scales%d" % place, pool_scales, U8, place) for place in range(last)]
+        scales_low = gather("scales3low", pool_scales, U8, last, None, 0, H)
+        for place in range(last):
+            cast_weights(place)
+            quantise_weights(place)
+            words = gather("words%d" % place, pool_words, U16, place, 2 * place * SLOT if place else None)
+            for q in range(QUARTERS):
+                multiply(place, q, words, scales[place], 0)
         cast_weights(last)
-        for t in range(PACK):
-            cols = slice(t * P, (t + 1) * P)
-            quantise(w_mx[last][0][:, cols], w_mx[last][1][:, cols], dealt[last][:, t, :, :].rearrange("p m r -> p (m r)"))
-            multiply(last, words3, scales3, t)
+        words_low = gather("words3low", pool_words, U16, last, (2 * last - 1) * SLOT, 0, H)
+        quantise_weights(last)
+        for q in range(2):
+            multiply(last, q, words_low, scales_low, 0)
+        end_slot = (2 * last + 1) * SLOT
+        words_high = gather("words3high", pool_words, U16, last, end_slot, H, H)
+        scales_high = gather("scales3high", pool_scales, U8, last, end_slot + 2 * H, H, H)
+        for q in range(2, QUARTERS):
+            multiply(last, q, words_high, scales_high, H)
 
-        grouped_wo = keep.tile([P, D, PACK], BF16, name="grouped_wo", tag="raw32", align_bytes=64)
-        for cols, copy in ((slice(0, D // 2), nc.scalar.copy), (slice(D // 2, D), nc.vector.tensor_copy)):
-            copy(
-                out=grouped_wo[:, cols, :].rearrange("p (c i) r -> p c r i", i=RUN),
-                in_=raw_wo[:, :, cols].rearrange("p r (c i) -> p c r i", i=RUN),
-            )
+        grouped_wo = stage.tile([P, D, PACK], BF16, name="grouped_wo", align_bytes=64, offset=end_slot + 4 * H)
+        nc.scalar.copy(
+            out=grouped_wo[:].rearrange("p (c i) r -> p c r i", i=RUN),
+            in_=raw_wo[:].rearrange("p r (c i) -> p c r i", i=RUN),
+        )
         wo_codes, wo_scales = mx_tiles("wo", D)
         quantise(wo_codes[:], wo_scales[:], grouped_wo[:].rearrange("p d r -> p (d r)"))
 
-        act = [keep.tile([P, J], F32, name="act%d" % t) for t in range(PACK)]
-        pairs = keep.tile([P, J * PACK], BF16, name="pairs", align_bytes=64)
-        pair_view = pairs[:].rearrange("p (h u j e) -> p h u j e", h=2, u=2, e=2)
-
-        def scale_by_gain(t, halves):
-            values = act[t][:].rearrange("p (h j) -> p h j", h=2)[:, halves, :]
-            nc.vector.tensor_scalar(
-                out=pair_view[:, halves, t // 2, :, t % 2], in0=values, scalar1=gains[:, t : t + 1], scalar2=None, op0=MULT
-            )
-
-        def keep_tensor_busy(t):
-            spare = psum.tile([P, J], F32, name="spare%d" % t, tag="z%d" % t)
-            nc.tensor.matmul_mx(
-                out=spare[:],
-                lhsT=w_mx[last][0][:, 0:P].bitcast(FP8X4),
-                lhsT_scale=w_mx[last][1][:, 0:P],
-                rhs=words3[:].bitcast(FP4X4),
-                rhs_scale=scales3[:],
-                start=True,
-                stop=True,
-            )
-
-        for t in range(2):
-            nc.scalar.activation(out=act[t][:], in_=z[t][:], func=GELU)
-            keep_tensor_busy(t)
-            scale_by_gain(t, slice(0, 2))
-        for h in range(2):
-            for t in range(2, PACK):
-                cols = slice(h * H, (h + 1) * H)
-                nc.scalar.activation(out=act[t][:, cols], in_=z[t][:, cols], func=GELU)
-                scale_by_gain(t, slice(h, h + 1))
-        for t in range(2, PACK):
-            keep_tensor_busy(t)
-
+        acts = []
+        for q in range(QUARTERS):
+            act = keep.tile([P, Q, PACK], F32, name="act%d" % q, align_bytes=64)
+            nc.scalar.activation(out=act[:], in_=z[q][:].rearrange("p t j -> p j t"), func=GELU)
+            acts.append(act)
         g_mx = []
-        for h, copy in enumerate((nc.scalar.copy, nc.vector.tensor_copy)):
-            g = keep.tile([P, H * PACK], BF16, name="g%d" % h, tag="g%d" % h, align_bytes=64)
-            copy(
-                out=g[:].bitcast(F32).rearrange("p (c i u) -> p c u i", i=RUN, u=2),
-                in_=pairs[:, h * H * PACK : (h + 1) * H * PACK].bitcast(F32).rearrange("p (u c i) -> p c u i", u=2, i=RUN),
-            )
-            g_mx.append(mx_tiles("g%d" % h, H))
-            quantise(g_mx[h][0][:], g_mx[h][1][:], g[:])
-
-        for h in range(2):
-            for block, copy in enumerate((nc.scalar.copy, nc.vector.tensor_copy)):
+        for q in range(QUARTERS):
+            g = keep.tile([P, Q, PACK], BF16, name="g%d" % q, align_bytes=64)
+            nc.vector.tensor_tensor(out=g[:], in0=acts[q][:], in1=gains[:].unsqueeze(1).to_broadcast([P, Q, PACK]), op=MULT)
+            g_mx.append(mx_tiles("g%d" % q, Q))
+            quantise(g_mx[q][0][:], g_mx[q][1][:], g[:].rearrange("p j t -> p (j t)"))
+        for q in range(QUARTERS):
+            y = psum.tile([P, 2, Q], F32, name="y%d" % q)
+            for block in range(2):
                 rows = slice(block * P, (block + 1) * P)
-                y = psum.tile([P, H], F32, name="y%d%d" % (h, block))
                 nc.tensor.matmul_mx(
-                    out=y[:],
+                    out=y[:, block, :],
                     lhsT=wo_codes[:, rows].bitcast(FP8X4),
                     lhsT_scale=wo_scales[:, rows],
-                    rhs=g_mx[h][0][:].bitcast(FP8X4),
-                    rhs_scale=g_mx[h][1][:],
+                    rhs=g_mx[q][0][:].bitcast(FP8X4),
+                    rhs_scale=g_mx[q][1][:],
                     start=True,
                     stop=True,
                 )
-                name = "result%d%d" % (h, block)
-                result = keep.tile([P, H], F32, name=name, tag="g1" if (h, block) == (0, 1) else name, align_bytes=64)
-                copy(out=result[:], in_=y[:])
-                nc.sync.dma_start(out=out[rows, h * H : (h + 1) * H], in_=result[:])
+            result = keep.tile([P, 2, Q], F32, name="result%d" % q, align_bytes=64)
+            nc.scalar.copy(out=result[:], in_=y[:])
+            nc.sync.dma_start(out=out.rearrange("(b p) j -> p b j", p=P)[:, :, q * Q : (q + 1) * Q], in_=result[:])

@@ -26,10 +26,8 @@ FP4X4 = mybir.dt.float4_e2m1fn_x4
 GELU = mybir.ActivationFunctionType.Gelu_apprx_tanh
 MULT = mybir.AluOpType.mult
 
-SLOT = PACK * (F // 2) * 4
-HALVES = (slice(0, F // 2), slice(F // 2, F))
-FIRST_PIECES = (slice(0, F // 4), slice(F // 4, F))
-W_PIECES = (FIRST_PIECES, HALVES, HALVES, HALVES)
+COLUMN_BYTES = PACK * 4
+PIECES = (((0, 256), (256, 512)),) * 4
 
 
 def tile_attend_nsa_compress_kernel(tc, tok_words, tok_scales, w0, w1, w2, w3, gain, wo, offs, offs2, offs3, offs4, out):
@@ -39,14 +37,22 @@ def tile_attend_nsa_compress_kernel(tc, tok_words, tok_scales, w0, w1, w2, w3, g
     last = PLACES - 1
     with ExitStack() as ctx:
         keep = ctx.enter_context(tc.tile_pool(name="keep", bufs=1))
+        stage = ctx.enter_context(tc.tile_pool(name="stage", bufs=1))
         psum = ctx.enter_context(tc.psum_pool(name="psum", bufs=1))
 
-        stage = ctx.enter_context(tc.tile_pool(name="stage", bufs=1))
+        def place_of(place, column):
+            return (place * F + column) * COLUMN_BYTES
 
-        def load_columns(name, matrix, cols, slot):
-            raw = stage.tile([P, PACK, cols.stop - cols.start], F32, name=name, align_bytes=64, offset=slot)
-            nc.sync.dma_start(out=raw[:], in_=matrix.rearrange("(p r) c -> p r c", r=PACK)[:, :, cols])
-            return raw
+        raw = {}
+
+        def load_piece(place, n):
+            first, end = PIECES[place][n]
+            tile = stage.tile([P, PACK, end - first], F32, name="raw%d%d" % (place, n), align_bytes=64, offset=place_of(place, first))
+            nc.sync.dma_start(out=tile[:], in_=weights[place].rearrange("(p r) c -> p r c", r=PACK)[:, :, first:end])
+            raw[place, n] = tile
+
+        def load_list(place):
+            nc.sync.dma_start(offsets[place][:], lists[place])
 
         def mx_tiles(name, width):
             codes = keep.tile([P, width], U32, name=name + "_codes", align_bytes=64)
@@ -60,42 +66,43 @@ def tile_attend_nsa_compress_kernel(tc, tok_words, tok_scales, w0, w1, w2, w3, g
         pool_scales = keep.tile([P, T], U8, name="pool_scales", align_bytes=64)
         offsets = [keep.tile([P, J // LIST_ROWS], U16, name="offsets%d" % place) for place in range(PLACES)]
         rows_in_quadrant = SCALE_ROWS * QUADRANT // P
-        nc.vector.memset(pool_scales[:, 0 : T // 2].bitcast(I32), 0)
-        nc.gpsimd.memset(pool_scales[:, T // 2 : T].bitcast(I32), 0)
-        for place in range(2):
-            nc.sync.dma_start(offsets[place][:], lists[place])
+        nc.vector.memset(pool_scales[:].bitcast(I32), 0)
         warm_in = keep.tile([P, 1], F32, name="warm_in")
         nc.vector.memset(warm_in[:], 0.0)
         warm_out = keep.tile([P, 1], F32, name="warm_out")
         nc.scalar.activation(out=warm_out[:], in_=warm_in[:], func=GELU)
 
-        raw = {}
+        def load_scales():
+            for r in range(rows_in_quadrant):
+                nc.sync.dma_start(
+                    out=pool_scales[r:P:QUADRANT, :].bitcast(I32),
+                    in_=tok_scales[0, r:SCALE_ROWS:rows_in_quadrant, :].bitcast(I32),
+                )
 
-        def load_half(place, n):
-            raw[place, n] = load_columns("raw%d%d" % (place, n), weights[place], W_PIECES[place][n], 2 * place * SLOT + PACK * 4 * W_PIECES[place][n].start)
+        def load_words():
+            nc.sync.dma_start(out=pool_words[:].bitcast(I32), in_=tok_words[0].bitcast(I32))
 
-        load_half(0, 0)
-        for r in range(rows_in_quadrant):
-            nc.sync.dma_start(
-                out=pool_scales[r:P:QUADRANT, :].bitcast(I32),
-                in_=tok_scales[0, r:SCALE_ROWS:rows_in_quadrant, :].bitcast(I32),
-            )
-        load_half(0, 1)
-        nc.sync.dma_start(offsets[2][:], lists[2])
-        load_half(1, 0)
-        nc.sync.dma_start(offsets[3][:], lists[3])
-        nc.sync.dma_start(out=pool_words[:].bitcast(I32), in_=tok_words[0].bitcast(I32))
-        load_half(1, 1)
+        load_list(0)
+        load_words()
+        load_scales()
+        load_list(1)
+        load_piece(0, 0)
+        load_piece(0, 1)
+        load_list(2)
+        load_piece(1, 0)
+        load_list(3)
+        load_piece(1, 1)
         for place in (2, 3):
-            for n in range(2):
-                load_half(place, n)
-        raw_wo = load_columns("raw_wo", wo, slice(0, D), 2 * PLACES * SLOT)
+            for n in range(len(PIECES[place])):
+                load_piece(place, n)
+        raw_wo = keep.tile([P, PACK, D], F32, name="raw_wo", align_bytes=64)
+        nc.sync.dma_start(out=raw_wo[:], in_=wo.rearrange("(p r) c -> p r c", r=PACK))
         gains = keep.tile([P, PACK], F32, name="gains")
         nc.sync.dma_start(out=gains[:], in_=gain.rearrange("(p t) o -> p (t o)", t=PACK))
 
         dealt = [keep.tile([P, PACK, P, PACK], BF16, name="dealt%d" % place, align_bytes=64) for place in range(PLACES)]
         w_mx = [mx_tiles("w%d" % place, F) for place in range(PLACES)]
-        z = [psum.tile([P, PACK, Q], F32, name="z%d" % q) for q in range(QUARTERS)]
+        z = [psum.tile([P, PACK, Q], F32, name="z%d" % q, tag="z%d" % q) for q in range(QUARTERS)]
 
         def gather(name, window, dtype, place, at=None, first=0, count=J):
             if at is None:
@@ -106,51 +113,68 @@ def tile_attend_nsa_compress_kernel(tc, tok_words, tok_scales, w0, w1, w2, w3, g
             nc.vector.tensor_copy(out=picked[:], in_=window[:].indirect(entries))
             return picked
 
+        def cast_piece(place, n, copy):
+            first, end = PIECES[place][n]
+            m = slice(first // PACK, end // PACK)
+            copy(
+                out=dealt[place][:, :, m, :].rearrange("p t m r -> p m r t"),
+                in_=raw[place, n][:].rearrange("p r (m t) -> p m r t", t=PACK),
+            )
+
         def cast_weights(place):
-            for n, cols in enumerate(W_PIECES[place]):
-                m = slice(cols.start // PACK, cols.stop // PACK)
-                nc.scalar.copy(
-                    out=dealt[place][:, :, m, :].rearrange("p t m r -> p m r t"),
-                    in_=raw[place, n][:].rearrange("p r (m t) -> p m r t", t=PACK),
-                )
+            for n in range(len(PIECES[place])):
+                cast_piece(place, n, nc.scalar.copy)
 
-        def quantise_weights(place):
-            quantise(w_mx[place][0][:], w_mx[place][1][:], dealt[place][:].rearrange("p t m r -> p (t m r)"))
+        def quantise_weights(place, tiles=slice(0, PACK)):
+            cols = slice(tiles.start * P, tiles.stop * P)
+            quantise(w_mx[place][0][:, cols], w_mx[place][1][:, cols], dealt[place][:, tiles, :, :].rearrange("p t m r -> p (t m r)"))
 
-        def multiply(place, q, words, scales, first):
+        def multiply(place, q, words, scales):
             for t in range(PACK):
                 cols = slice(t * P, (t + 1) * P)
-                blocks = slice(q * Q - first, (q + 1) * Q - first)
                 nc.tensor.matmul_mx(
                     out=z[q][:, t, :],
                     lhsT=w_mx[place][0][:, cols].bitcast(FP8X4),
                     lhsT_scale=w_mx[place][1][:, cols],
-                    rhs=words[:, blocks].bitcast(FP4X4),
-                    rhs_scale=scales[:, blocks],
+                    rhs=words.bitcast(FP4X4),
+                    rhs_scale=scales,
                     start=(place == 0 and t == 0),
                     stop=(place == last and t == PACK - 1),
                 )
 
-        scales = [gather("scales%d" % place, pool_scales, U8, place) for place in range(last)]
-        scales_low = gather("scales3low", pool_scales, U8, last, None, 0, H)
-        for place in range(last):
-            cast_weights(place)
-            quantise_weights(place)
-            words = gather("words%d" % place, pool_words, U16, place, 2 * place * SLOT if place else None)
-            for q in range(QUARTERS):
-                multiply(place, q, words, scales[place], 0)
-        cast_weights(last)
-        words_low = gather("words3low", pool_words, U16, last, (2 * last - 1) * SLOT, 0, H)
-        quantise_weights(last)
-        for q in range(2):
-            multiply(last, q, words_low, scales_low, 0)
-        end_slot = (2 * last + 1) * SLOT
-        words_high = gather("words3high", pool_words, U16, last, end_slot, H, H)
-        scales_high = gather("scales3high", pool_scales, U8, last, end_slot + 2 * H, H, H)
-        for q in range(2, QUARTERS):
-            multiply(last, q, words_high, scales_high, H)
+        def quarter(tile, q):
+            return tile[:, q * Q : (q + 1) * Q]
 
-        grouped_wo = stage.tile([P, D, PACK], BF16, name="grouped_wo", align_bytes=64, offset=end_slot + 4 * H)
+        words, scales = {}, {}
+        for place in range(2):
+            words[place] = gather("words%d" % place, pool_words, U16, place)
+            scales[place] = gather("scales%d" % place, pool_scales, U8, place)
+
+        def passes(place, quarters, first=0):
+            for q in quarters:
+                multiply(place, q, quarter(words[place], q - first), quarter(scales[place], q - first))
+
+        cast_weights(0)
+        quantise_weights(0)
+        passes(0, range(QUARTERS))
+        words[2] = gather("words2", pool_words, U16, 2, place_of(0, 256))
+        cast_weights(1)
+        quantise_weights(1)
+        passes(1, range(QUARTERS))
+        scales[2] = gather("scales2", pool_scales, U8, 2, place_of(1, 256))
+        cast_weights(2)
+        quantise_weights(2)
+        passes(2, range(QUARTERS))
+        words[last] = gather("words3low", pool_words, U16, last, place_of(2, 256), 0, H)
+        scales[last] = gather("scales3low", pool_scales, U8, last, place_of(2, 256) + 2 * H, 0, H)
+        cast_weights(last)
+        quantise_weights(last)
+        passes(last, range(2))
+        words[last] = gather("words3high", pool_words, U16, last, place_of(last, 256), H, H)
+        scales[last] = gather("scales3high", pool_scales, U8, last, place_of(last, 256) + 2 * H, H, H)
+        passes(last, range(2, QUARTERS), 2)
+
+        grouped_wo = stage.tile([P, D, PACK], BF16, name="grouped_wo", align_bytes=64, offset=place_of(last, 256) + 4 * H)
         nc.scalar.copy(
             out=grouped_wo[:].rearrange("p (c i) r -> p c r i", i=RUN),
             in_=raw_wo[:].rearrange("p r (c i) -> p c r i", i=RUN),
@@ -163,12 +187,13 @@ def tile_attend_nsa_compress_kernel(tc, tok_words, tok_scales, w0, w1, w2, w3, g
             act = keep.tile([P, Q, PACK], F32, name="act%d" % q, align_bytes=64)
             nc.scalar.activation(out=act[:], in_=z[q][:].rearrange("p t j -> p j t"), func=GELU)
             acts.append(act)
-        g_mx = []
-        for q in range(QUARTERS):
-            g = keep.tile([P, Q, PACK], BF16, name="g%d" % q, align_bytes=64)
-            nc.vector.tensor_tensor(out=g[:], in0=acts[q][:], in1=gains[:].unsqueeze(1).to_broadcast([P, Q, PACK]), op=MULT)
-            g_mx.append(mx_tiles("g%d" % q, Q))
-            quantise(g_mx[q][0][:], g_mx[q][1][:], g[:].rearrange("p j t -> p (j t)"))
+        g = [keep.tile([P, Q, PACK], BF16, name="g%d" % q, align_bytes=64) for q in range(QUARTERS)]
+        g_mx = [mx_tiles("g%d" % q, Q) for q in range(QUARTERS)]
+        for step in range(QUARTERS + 1):
+            if step < QUARTERS:
+                nc.vector.tensor_tensor(out=g[step][:], in0=acts[step][:], in1=gains[:].unsqueeze(1).to_broadcast([P, Q, PACK]), op=MULT)
+            if step > 0:
+                quantise(g_mx[step - 1][0][:], g_mx[step - 1][1][:], g[step - 1][:].rearrange("p j t -> p (j t)"))
         for q in range(QUARTERS):
             y = psum.tile([P, 2, Q], F32, name="y%d" % q)
             for block in range(2):

@@ -168,7 +168,8 @@ def tile_attend_nsa_compress_kernel(tc, tok_words, tok_scales, w0, w1, w2, w3, g
         words[last] = gather("words3low", pool_words, U16, last, place_of(2, 256), 0, H)
         scales[last] = gather("scales3low", pool_scales, U8, last, place_of(2, 256) + 2 * H, 0, H)
         cast_weights(last)
-        quantise_weights(last)
+        for t in range(PACK):
+            quantise_weights(last, slice(t, t + 1))
         passes(last, range(2))
         words[last] = gather("words3high", pool_words, U16, last, place_of(last, 256), H, H)
         scales[last] = gather("scales3high", pool_scales, U8, last, place_of(last, 256) + 2 * H, H, H)
@@ -187,26 +188,41 @@ def tile_attend_nsa_compress_kernel(tc, tok_words, tok_scales, w0, w1, w2, w3, g
             act = keep.tile([P, Q, PACK], F32, name="act%d" % q, align_bytes=64)
             nc.scalar.activation(out=act[:], in_=z[q][:].rearrange("p t j -> p j t"), func=GELU)
             acts.append(act)
-        g = [keep.tile([P, Q, PACK], BF16, name="g%d" % q, align_bytes=64) for q in range(QUARTERS)]
-        g_mx = [mx_tiles("g%d" % q, Q) for q in range(QUARTERS)]
-        for step in range(QUARTERS + 1):
-            if step < QUARTERS:
-                nc.vector.tensor_tensor(out=g[step][:], in0=acts[step][:], in1=gains[:].unsqueeze(1).to_broadcast([P, Q, PACK]), op=MULT)
+            if q > 0:
+                spare = psum.tile([P, J], F32, name="spare%d" % q, tag="z%d" % q)
+                nc.tensor.matmul_mx(
+                    out=spare[:],
+                    lhsT=w_mx[0][0][:, 0:P].bitcast(FP8X4),
+                    lhsT_scale=w_mx[0][1][:, 0:P],
+                    rhs=words[0][:].bitcast(FP4X4),
+                    rhs_scale=scales[0][:],
+                    start=True,
+                    stop=True,
+                )
+        spans = ((0, 128), (128, 128), (256, 128), (384, 128))
+        g = [keep.tile([P, count, PACK], BF16, name="g%d" % n, align_bytes=64) for n, (first, count) in enumerate(spans)]
+        g_mx = [mx_tiles("g%d" % n, count) for n, (first, count) in enumerate(spans)]
+        for step in range(len(spans) + 1):
+            if step < len(spans):
+                first, count = spans[step]
+                act = acts[first // Q][:, first % Q : first % Q + count, :]
+                nc.vector.tensor_tensor(out=g[step][:], in0=act, in1=gains[:].unsqueeze(1).to_broadcast([P, count, PACK]), op=MULT)
             if step > 0:
                 quantise(g_mx[step - 1][0][:], g_mx[step - 1][1][:], g[step - 1][:].rearrange("p j t -> p (j t)"))
-        for q in range(QUARTERS):
-            y = psum.tile([P, 2, Q], F32, name="y%d" % q)
+        for n, (first, count) in enumerate(spans):
+            y = psum.tile([P, 2, count], F32, name="y%d" % n, tag="y%d" % n if n < QUARTERS else "z%d" % (n - QUARTERS))
             for block in range(2):
                 rows = slice(block * P, (block + 1) * P)
                 nc.tensor.matmul_mx(
                     out=y[:, block, :],
                     lhsT=wo_codes[:, rows].bitcast(FP8X4),
                     lhsT_scale=wo_scales[:, rows],
-                    rhs=g_mx[q][0][:].bitcast(FP8X4),
-                    rhs_scale=g_mx[q][1][:],
+                    rhs=g_mx[n][0][:].bitcast(FP8X4),
+                    rhs_scale=g_mx[n][1][:],
                     start=True,
                     stop=True,
                 )
-            result = keep.tile([P, 2, Q], F32, name="result%d" % q, align_bytes=64)
-            nc.scalar.copy(out=result[:], in_=y[:])
-            nc.sync.dma_start(out=out.rearrange("(b p) j -> p b j", p=P)[:, :, q * Q : (q + 1) * Q], in_=result[:])
+            result = keep.tile([P, 2, count], F32, name="result%d" % n, align_bytes=64)
+            copy = nc.vector.tensor_copy if n >= len(spans) - 1 else nc.scalar.copy
+            copy(out=result[:], in_=y[:])
+            nc.sync.dma_start(out=out.rearrange("(b p) j -> p b j", p=P)[:, :, first : first + count], in_=result[:])

@@ -188,17 +188,6 @@ def tile_attend_nsa_compress_kernel(tc, tok_words, tok_scales, w0, w1, w2, w3, g
             act = keep.tile([P, Q, PACK], F32, name="act%d" % q, align_bytes=64)
             nc.scalar.activation(out=act[:], in_=z[q][:].rearrange("p t j -> p j t"), func=GELU)
             acts.append(act)
-            if q > 0:
-                spare = psum.tile([P, J], F32, name="spare%d" % q, tag="z%d" % q)
-                nc.tensor.matmul_mx(
-                    out=spare[:],
-                    lhsT=w_mx[0][0][:, 0:P].bitcast(FP8X4),
-                    lhsT_scale=w_mx[0][1][:, 0:P],
-                    rhs=words[0][:].bitcast(FP4X4),
-                    rhs_scale=scales[0][:],
-                    start=True,
-                    stop=True,
-                )
         spans = ((0, 128), (128, 128), (256, 128), (384, 128))
         g = [keep.tile([P, count, PACK], BF16, name="g%d" % n, align_bytes=64) for n, (first, count) in enumerate(spans)]
         g_mx = [mx_tiles("g%d" % n, count) for n, (first, count) in enumerate(spans)]

@@ -26,8 +26,9 @@ FP4X4 = mybir.dt.float4_e2m1fn_x4
 GELU = mybir.ActivationFunctionType.Gelu_apprx_tanh
 MULT = mybir.AluOpType.mult
 
-COLUMN_BYTES = PACK * 4
-PIECES = (((0, 256), (256, 512)),) * 4
+HALVES = (slice(0, F // 2), slice(F // 2, F))
+HALF_BYTES = PACK * (F // 2) * 4
+WORD_BYTES = 2
 
 
 def tile_attend_nsa_compress_kernel(tc, tok_words, tok_scales, w0, w1, w2, w3, gain, wo, offs, offs2, offs3, offs4, out):
@@ -40,61 +41,55 @@ def tile_attend_nsa_compress_kernel(tc, tok_words, tok_scales, w0, w1, w2, w3, g
         stage = ctx.enter_context(tc.tile_pool(name="stage", bufs=1))
         psum = ctx.enter_context(tc.psum_pool(name="psum", bufs=1))
 
-        def place_of(place, column):
-            return (place * F + column) * COLUMN_BYTES
+        def staged_at(place, half):
+            return (len(HALVES) * place + half) * HALF_BYTES
 
         raw = {}
 
-        def load_piece(place, n):
-            first, end = PIECES[place][n]
-            tile = stage.tile([P, PACK, end - first], F32, name="raw%d%d" % (place, n), align_bytes=64, offset=place_of(place, first))
-            nc.sync.dma_start(out=tile[:], in_=weights[place].rearrange("(p r) c -> p r c", r=PACK)[:, :, first:end])
-            raw[place, n] = tile
+        def load_half(place, half):
+            tile = stage.tile([P, PACK, F // 2], F32, name="raw%d%d" % (place, half), align_bytes=64, offset=staged_at(place, half))
+            nc.sync.dma_start(out=tile[:], in_=weights[place].rearrange("(p r) c -> p r c", r=PACK)[:, :, HALVES[half]])
+            raw[place, half] = tile
 
         def load_list(place):
             nc.sync.dma_start(offsets[place][:], lists[place])
 
         def mx_tiles(name, width):
             codes = keep.tile([P, width], U32, name=name + "_codes", align_bytes=64)
-            scales = keep.tile([P, width], U8, name=name + "_scales", align_bytes=64)
-            return codes, scales
+            scale_bytes = keep.tile([P, width], U8, name=name + "_scales", align_bytes=64)
+            return codes, scale_bytes
 
-        def quantise(codes, scales, values):
-            nc.vector.quantize_mx(out=codes.bitcast(FP8X4), scales=scales, in_=values)
+        def quantise(codes, scale_bytes, values):
+            nc.vector.quantize_mx(out=codes.bitcast(FP8X4), scales=scale_bytes, in_=values)
 
         pool_words = keep.tile([P, T], U16, name="pool_words", align_bytes=64)
         pool_scales = keep.tile([P, T], U8, name="pool_scales", align_bytes=64)
         offsets = [keep.tile([P, J // LIST_ROWS], U16, name="offsets%d" % place) for place in range(PLACES)]
         rows_in_quadrant = SCALE_ROWS * QUADRANT // P
         nc.vector.memset(pool_scales[:].bitcast(I32), 0)
+
         warm_in = keep.tile([P, 1], F32, name="warm_in")
         nc.vector.memset(warm_in[:], 0.0)
         warm_out = keep.tile([P, 1], F32, name="warm_out")
         nc.scalar.activation(out=warm_out[:], in_=warm_in[:], func=GELU)
 
-        def load_scales():
-            for r in range(rows_in_quadrant):
-                nc.sync.dma_start(
-                    out=pool_scales[r:P:QUADRANT, :].bitcast(I32),
-                    in_=tok_scales[0, r:SCALE_ROWS:rows_in_quadrant, :].bitcast(I32),
-                )
-
-        def load_words():
-            nc.sync.dma_start(out=pool_words[:].bitcast(I32), in_=tok_words[0].bitcast(I32))
-
         load_list(0)
-        load_words()
-        load_scales()
+        nc.sync.dma_start(out=pool_words[:].bitcast(I32), in_=tok_words[0].bitcast(I32))
+        for r in range(rows_in_quadrant):
+            nc.sync.dma_start(
+                out=pool_scales[r:P:QUADRANT, :].bitcast(I32),
+                in_=tok_scales[0, r:SCALE_ROWS:rows_in_quadrant, :].bitcast(I32),
+            )
         load_list(1)
-        load_piece(0, 0)
-        load_piece(0, 1)
+        load_half(0, 0)
+        load_half(0, 1)
         load_list(2)
-        load_piece(1, 0)
+        load_half(1, 0)
         load_list(3)
-        load_piece(1, 1)
-        for place in (2, 3):
-            for n in range(len(PIECES[place])):
-                load_piece(place, n)
+        load_half(1, 1)
+        for place in range(2, PLACES):
+            for half in range(len(HALVES)):
+                load_half(place, half)
         raw_wo = keep.tile([P, PACK, D], F32, name="raw_wo", align_bytes=64)
         nc.sync.dma_start(out=raw_wo[:], in_=wo.rearrange("(p r) c -> p r c", r=PACK))
         gains = keep.tile([P, PACK], F32, name="gains")
@@ -113,69 +108,62 @@ def tile_attend_nsa_compress_kernel(tc, tok_words, tok_scales, w0, w1, w2, w3, g
             nc.vector.tensor_copy(out=picked[:], in_=window[:].indirect(entries))
             return picked
 
-        def cast_piece(place, n, copy):
-            first, end = PIECES[place][n]
-            m = slice(first // PACK, end // PACK)
-            copy(
-                out=dealt[place][:, :, m, :].rearrange("p t m r -> p m r t"),
-                in_=raw[place, n][:].rearrange("p r (m t) -> p m r t", t=PACK),
-            )
-
         def cast_weights(place):
-            for n in range(len(PIECES[place])):
-                cast_piece(place, n, nc.scalar.copy)
-
-        def quantise_weights(place, tiles=slice(0, PACK)):
-            cols = slice(tiles.start * P, tiles.stop * P)
-            quantise(w_mx[place][0][:, cols], w_mx[place][1][:, cols], dealt[place][:, tiles, :, :].rearrange("p t m r -> p (t m r)"))
-
-        def multiply(place, q, words, scales):
-            for t in range(PACK):
-                cols = slice(t * P, (t + 1) * P)
-                nc.tensor.matmul_mx(
-                    out=z[q][:, t, :],
-                    lhsT=w_mx[place][0][:, cols].bitcast(FP8X4),
-                    lhsT_scale=w_mx[place][1][:, cols],
-                    rhs=words.bitcast(FP4X4),
-                    rhs_scale=scales,
-                    start=(place == 0 and t == 0),
-                    stop=(place == last and t == PACK - 1),
+            for half, cols in enumerate(HALVES):
+                m = slice(cols.start // PACK, cols.stop // PACK)
+                nc.scalar.copy(
+                    out=dealt[place][:, :, m, :].rearrange("p t m r -> p m r t"),
+                    in_=raw[place, half][:].rearrange("p r (m t) -> p m r t", t=PACK),
                 )
 
-        def quarter(tile, q):
-            return tile[:, q * Q : (q + 1) * Q]
+        def quantise_weights(place):
+            quantise(w_mx[place][0][:], w_mx[place][1][:], dealt[place][:].rearrange("p t m r -> p (t m r)"))
 
         words, scales = {}, {}
+
+        def multiply(place, quarters):
+            for n, q in enumerate(quarters):
+                blocks = slice(n * Q, (n + 1) * Q)
+                for t in range(PACK):
+                    cols = slice(t * P, (t + 1) * P)
+                    nc.tensor.matmul_mx(
+                        out=z[q][:, t, :],
+                        lhsT=w_mx[place][0][:, cols].bitcast(FP8X4),
+                        lhsT_scale=w_mx[place][1][:, cols],
+                        rhs=words[place][:, blocks].bitcast(FP4X4),
+                        rhs_scale=scales[place][:, blocks],
+                        start=(place == 0 and t == 0),
+                        stop=(place == last and t == PACK - 1),
+                    )
+
         for place in range(2):
             words[place] = gather("words%d" % place, pool_words, U16, place)
             scales[place] = gather("scales%d" % place, pool_scales, U8, place)
-
-        def passes(place, quarters, first=0):
-            for q in quarters:
-                multiply(place, q, quarter(words[place], q - first), quarter(scales[place], q - first))
-
         cast_weights(0)
         quantise_weights(0)
-        passes(0, range(QUARTERS))
-        words[2] = gather("words2", pool_words, U16, 2, place_of(0, 256))
+        multiply(0, range(QUARTERS))
+        words[2] = gather("words2", pool_words, U16, 2, staged_at(0, 1))
         cast_weights(1)
         quantise_weights(1)
-        passes(1, range(QUARTERS))
-        scales[2] = gather("scales2", pool_scales, U8, 2, place_of(1, 256))
+        multiply(1, range(QUARTERS))
+        scales[2] = gather("scales2", pool_scales, U8, 2, staged_at(1, 1))
         cast_weights(2)
         quantise_weights(2)
-        passes(2, range(QUARTERS))
-        words[last] = gather("words3low", pool_words, U16, last, place_of(2, 256), 0, H)
-        scales[last] = gather("scales3low", pool_scales, U8, last, place_of(2, 256) + 2 * H, 0, H)
+        multiply(2, range(QUARTERS))
+        words[last] = gather("words3low", pool_words, U16, last, staged_at(2, 1), 0, H)
+        scales[last] = gather("scales3low", pool_scales, U8, last, staged_at(2, 1) + WORD_BYTES * H, 0, H)
         cast_weights(last)
-        for t in range(PACK):
-            quantise_weights(last, slice(t, t + 1))
-        passes(last, range(2))
-        words[last] = gather("words3high", pool_words, U16, last, place_of(last, 256), H, H)
-        scales[last] = gather("scales3high", pool_scales, U8, last, place_of(last, 256) + 2 * H, H, H)
-        passes(last, range(2, QUARTERS), 2)
+        for half in range(len(HALVES)):
+            for t in range(PACK):
+                m = slice(half * P // 2, (half + 1) * P // 2)
+                cols = slice(t * P + m.start, t * P + m.stop)
+                quantise(w_mx[last][0][:, cols], w_mx[last][1][:, cols], dealt[last][:, t, m, :].rearrange("p m r -> p (m r)"))
+        multiply(last, range(QUARTERS // 2))
+        words[last] = gather("words3high", pool_words, U16, last, staged_at(last, 1), H, H)
+        scales[last] = gather("scales3high", pool_scales, U8, last, staged_at(last, 1) + WORD_BYTES * H, H, H)
+        multiply(last, range(QUARTERS // 2, QUARTERS))
 
-        grouped_wo = stage.tile([P, D, PACK], BF16, name="grouped_wo", align_bytes=64, offset=place_of(last, 256) + 4 * H)
+        grouped_wo = stage.tile([P, D, PACK], BF16, name="grouped_wo", align_bytes=64, offset=staged_at(last, 1) + 2 * WORD_BYTES * H)
         nc.scalar.copy(
             out=grouped_wo[:].rearrange("p (c i) r -> p c r i", i=RUN),
             in_=raw_wo[:].rearrange("p r (c i) -> p c r i", i=RUN),
@@ -188,30 +176,28 @@ def tile_attend_nsa_compress_kernel(tc, tok_words, tok_scales, w0, w1, w2, w3, g
             act = keep.tile([P, Q, PACK], F32, name="act%d" % q, align_bytes=64)
             nc.scalar.activation(out=act[:], in_=z[q][:].rearrange("p t j -> p j t"), func=GELU)
             acts.append(act)
-        spans = ((0, 128), (128, 128), (256, 128), (384, 128))
-        g = [keep.tile([P, count, PACK], BF16, name="g%d" % n, align_bytes=64) for n, (first, count) in enumerate(spans)]
-        g_mx = [mx_tiles("g%d" % n, count) for n, (first, count) in enumerate(spans)]
-        for step in range(len(spans) + 1):
-            if step < len(spans):
-                first, count = spans[step]
-                act = acts[first // Q][:, first % Q : first % Q + count, :]
-                nc.vector.tensor_tensor(out=g[step][:], in0=act, in1=gains[:].unsqueeze(1).to_broadcast([P, count, PACK]), op=MULT)
+        g = [keep.tile([P, Q, PACK], BF16, name="g%d" % q, align_bytes=64) for q in range(QUARTERS)]
+        g_mx = [mx_tiles("g%d" % q, Q) for q in range(QUARTERS)]
+        for step in range(QUARTERS + 1):
+            if step < QUARTERS:
+                nc.vector.tensor_tensor(out=g[step][:], in0=acts[step][:], in1=gains[:].unsqueeze(1).to_broadcast([P, Q, PACK]), op=MULT)
             if step > 0:
                 quantise(g_mx[step - 1][0][:], g_mx[step - 1][1][:], g[step - 1][:].rearrange("p j t -> p (j t)"))
-        for n, (first, count) in enumerate(spans):
-            y = psum.tile([P, 2, count], F32, name="y%d" % n, tag="y%d" % n if n < QUARTERS else "z%d" % (n - QUARTERS))
-            for block in range(2):
+
+        for q in range(QUARTERS):
+            y = psum.tile([P, D // P, Q], F32, name="y%d" % q, tag="y%d" % q)
+            for block in range(D // P):
                 rows = slice(block * P, (block + 1) * P)
                 nc.tensor.matmul_mx(
                     out=y[:, block, :],
                     lhsT=wo_codes[:, rows].bitcast(FP8X4),
                     lhsT_scale=wo_scales[:, rows],
-                    rhs=g_mx[n][0][:].bitcast(FP8X4),
-                    rhs_scale=g_mx[n][1][:],
+                    rhs=g_mx[q][0][:].bitcast(FP8X4),
+                    rhs_scale=g_mx[q][1][:],
                     start=True,
                     stop=True,
                 )
-            result = keep.tile([P, 2, count], F32, name="result%d" % n, align_bytes=64)
-            copy = nc.vector.tensor_copy if n >= len(spans) - 1 else nc.scalar.copy
+            result = keep.tile([P, D // P, Q], F32, name="result%d" % q, align_bytes=64)
+            copy = nc.vector.tensor_copy if q == QUARTERS - 1 else nc.scalar.copy
             copy(out=result[:], in_=y[:])
-            nc.sync.dma_start(out=out.rearrange("(b p) j -> p b j", p=P)[:, :, first : first + count], in_=result[:])
+            nc.sync.dma_start(out=out.rearrange("(b p) j -> p b j", p=P)[:, :, q * Q : (q + 1) * Q], in_=result[:])

@@ -75,12 +75,12 @@ def tile_attend_nsa_compress_kernel(tc, tok_words, tok_scales, w0, w1, w2, w3, g
 
         load_list(0)
         nc.sync.dma_start(out=pool_words[:].bitcast(I32), in_=tok_words[0].bitcast(I32))
+        load_list(1)
         for r in range(rows_in_quadrant):
             nc.sync.dma_start(
                 out=pool_scales[r:P:QUADRANT, :].bitcast(I32),
                 in_=tok_scales[0, r:SCALE_ROWS:rows_in_quadrant, :].bitcast(I32),
             )
-        load_list(1)
         load_half(0, 0)
         load_half(0, 1)
         load_list(2)
@@ -138,6 +138,7 @@ def tile_attend_nsa_compress_kernel(tc, tok_words, tok_scales, w0, w1, w2, w3, g
 
         for place in range(2):
             words[place] = gather("words%d" % place, pool_words, U16, place)
+        for place in range(2):
             scales[place] = gather("scales%d" % place, pool_scales, U8, place)
         cast_weights(0)
         quantise_weights(0)

@@ -25,6 +25,7 @@ FP8X4 = mybir.dt.float8_e4m3fn_x4
 FP4X4 = mybir.dt.float4_e2m1fn_x4
 GELU = mybir.ActivationFunctionType.Gelu_apprx_tanh
 MULT = mybir.AluOpType.mult
+ADD = mybir.AluOpType.add
 
 HALVES = (slice(0, F // 2), slice(F // 2, F))
 HALF_BYTES = PACK * (F // 2) * 4
@@ -111,6 +112,16 @@ def tile_attend_nsa_compress_kernel(tc, tok_words, tok_scales, w0, w1, w2, w3, g
         def cast_weights(place):
             for half, cols in enumerate(HALVES):
                 m = slice(cols.start // PACK, cols.stop // PACK)
+                if (place, half) == (0, 0):
+                    nc.gpsimd.tensor_scalar(
+                        out=dealt[place][:, :, m, :],
+                        in0=raw[place, half][:].rearrange("p r (m t) -> p t m r", t=PACK),
+                        scalar1=1.0,
+                        scalar2=0.0,
+                        op0=MULT,
+                        op1=ADD,
+                    )
+                    continue
                 nc.scalar.copy(
                     out=dealt[place][:, :, m, :].rearrange("p t m r -> p m r t"),
                     in_=raw[place, half][:].rearrange("p r (m t) -> p m r t", t=PACK),

@@ -50,7 +50,7 @@ def tile_attend_nsa_compress_kernel(tc, tok_words, tok_scales, w0, w1, w2, w3, g
         def load_half(place, half):
             tile = stage.tile([P, PACK, F // 2], F32, name="raw%d%d" % (place, half), align_bytes=64, offset=staged_at(place, half))
             nc.sync.dma_start(out=tile[:], in_=weights[place].rearrange("(p r) c -> p r c", r=PACK)[:, :, HALVES[half]])
-            raw[place, half] = tile
+            raw[place, half] = tile[:]
 
         def load_list(place):
             nc.sync.dma_start(offsets[place][:], lists[place])
@@ -82,13 +82,14 @@ def tile_attend_nsa_compress_kernel(tc, tok_words, tok_scales, w0, w1, w2, w3, g
                 out=pool_scales[r:P:QUADRANT, :].bitcast(I32),
                 in_=tok_scales[0, r:SCALE_ROWS:rows_in_quadrant, :].bitcast(I32),
             )
-        load_half(0, 0)
-        load_half(0, 1)
-        load_list(2)
+        whole = stage.tile([P, PACK, F], F32, name="raw0", align_bytes=64, offset=staged_at(0, 0))
+        nc.sync.dma_start(out=whole[:], in_=weights[0].rearrange("(p r) c -> p r c", r=PACK))
+        for half, cols in enumerate(HALVES):
+            raw[0, half] = whole[:, :, cols]
         load_half(1, 0)
-        load_list(3)
         load_half(1, 1)
         for place in range(2, PLACES):
+            load_list(place)
             for half in range(len(HALVES)):
                 load_half(place, half)
         raw_wo = keep.tile([P, PACK, D], F32, name="raw_wo", align_bytes=64)
@@ -115,7 +116,7 @@ def tile_attend_nsa_compress_kernel(tc, tok_words, tok_scales, w0, w1, w2, w3, g
                 if (place, half) == (0, 0):
                     nc.gpsimd.tensor_scalar(
                         out=dealt[place][:, :, m, :],
-                        in0=raw[place, half][:].rearrange("p r (m t) -> p t m r", t=PACK),
+                        in0=raw[place, half].rearrange("p r (m t) -> p t m r", t=PACK),
                         scalar1=1.0,
                         scalar2=0.0,
                         op0=MULT,
@@ -124,7 +125,7 @@ def tile_attend_nsa_compress_kernel(tc, tok_words, tok_scales, w0, w1, w2, w3, g
                     continue
                 nc.scalar.copy(
                     out=dealt[place][:, :, m, :].rearrange("p t m r -> p m r t"),
-                    in_=raw[place, half][:].rearrange("p r (m t) -> p m r t", t=PACK),
+                    in_=raw[place, half].rearrange("p r (m t) -> p m r t", t=PACK),
                 )
 
         def quantise_weights(place):

@@ -70,12 +70,12 @@ def tile_attend_nsa_compress_kernel(tc, tok_words, tok_scales, w0, w1, w2, w3, g
         nc.vector.memset(pool_scales[:].bitcast(I32), 0)
 
         warm_in = keep.tile([P, 1], F32, name="warm_in")
-        nc.vector.memset(warm_in[:], 0.0)
+        nc.gpsimd.memset(warm_in[:], 0.0)
         warm_out = keep.tile([P, 1], F32, name="warm_out")
         nc.scalar.activation(out=warm_out[:], in_=warm_in[:], func=GELU)
 
-        load_list(0)
         nc.sync.dma_start(out=pool_words[:].bitcast(I32), in_=tok_words[0].bitcast(I32))
+        load_list(0)
         load_list(1)
         for r in range(rows_in_quadrant):
             nc.sync.dma_start(
@@ -115,8 +115,8 @@ def tile_attend_nsa_compress_kernel(tc, tok_words, tok_scales, w0, w1, w2, w3, g
                 m = slice(cols.start // PACK, cols.stop // PACK)
                 if (place, half) == (0, 0):
                     nc.gpsimd.tensor_scalar(
-                        out=dealt[place][:, :, m, :],
-                        in0=raw[place, half].rearrange("p r (m t) -> p t m r", t=PACK),
+                        out=dealt[place][:, :, m, :].rearrange("p t m r -> p m t r"),
+                        in0=raw[place, half].rearrange("p r (m t) -> p m t r", t=PACK),
                         scalar1=1.0,
                         scalar2=0.0,
                         op0=MULT,
@@ -176,19 +176,26 @@ def tile_attend_nsa_compress_kernel(tc, tok_words, tok_scales, w0, w1, w2, w3, g
         scales[last] = gather("scales3high", pool_scales, U8, last, staged_at(last, 1) + WORD_BYTES * H, H, H)
         multiply(last, range(QUARTERS // 2, QUARTERS))
 
-        grouped_wo = stage.tile([P, D, PACK], BF16, name="grouped_wo", align_bytes=64, offset=staged_at(last, 1) + 2 * WORD_BYTES * H)
-        nc.scalar.copy(
-            out=grouped_wo[:].rearrange("p (c i) r -> p c r i", i=RUN),
-            in_=raw_wo[:].rearrange("p r (c i) -> p c r i", i=RUN),
-        )
         wo_codes, wo_scales = mx_tiles("wo", D)
-        quantise(wo_codes[:], wo_scales[:], grouped_wo[:].rearrange("p d r -> p (d r)"))
+
+        def prepare_wo(block, at):
+            cols = slice(block * P, (block + 1) * P)
+            grouped = stage.tile([P, P, PACK], BF16, name="grouped_wo%d" % block, align_bytes=64, offset=at)
+            nc.scalar.copy(
+                out=grouped[:].rearrange("p (c i) r -> p c r i", i=RUN),
+                in_=raw_wo[:, :, cols].rearrange("p r (c i) -> p c r i", i=RUN),
+            )
+            return lambda: quantise(wo_codes[:, cols], wo_scales[:, cols], grouped[:].rearrange("p d r -> p (d r)"))
+
+        prepare_wo(0, staged_at(last, 1) + 2 * WORD_BYTES * H)()
 
         acts = []
         for q in range(QUARTERS):
             act = keep.tile([P, Q, PACK], F32, name="act%d" % q, align_bytes=64)
             nc.scalar.activation(out=act[:], in_=z[q][:].rearrange("p t j -> p j t"), func=GELU)
             acts.append(act)
+            if q == QUARTERS // 2 - 1:
+                quantise_second_block = prepare_wo(1, staged_at(2, 1))
         g = [keep.tile([P, Q, PACK], BF16, name="g%d" % q, align_bytes=64) for q in range(QUARTERS)]
         g_mx = [mx_tiles("g%d" % q, Q) for q in range(QUARTERS)]
         for step in range(QUARTERS + 1):
@@ -196,6 +203,8 @@ def tile_attend_nsa_compress_kernel(tc, tok_words, tok_scales, w0, w1, w2, w3, g
                 nc.vector.tensor_tensor(out=g[step][:], in0=acts[step][:], in1=gains[:].unsqueeze(1).to_broadcast([P, Q, PACK]), op=MULT)
             if step > 0:
                 quantise(g_mx[step - 1][0][:], g_mx[step - 1][1][:], g[step - 1][:].rearrange("p j t -> p (j t)"))
+            if step == 1:
+                quantise_second_block()
 
         for q in range(QUARTERS):
             y = psum.tile([P, D // P, Q], F32, name="y%d" % q, tag="y%d" % q)

@@ -30,6 +30,7 @@ ADD = mybir.AluOpType.add
 HALVES = (slice(0, F // 2), slice(F // 2, F))
 HALF_BYTES = PACK * (F // 2) * 4
 WORD_BYTES = 2
+WO_EARLY = 3 * D // 4
 
 
 def tile_attend_nsa_compress_kernel(tc, tok_words, tok_scales, w0, w1, w2, w3, gain, wo, offs, offs2, offs3, offs4, out):
@@ -178,16 +179,20 @@ def tile_attend_nsa_compress_kernel(tc, tok_words, tok_scales, w0, w1, w2, w3, g
 
         wo_codes, wo_scales = mx_tiles("wo", D)
 
-        def prepare_wo(block, at):
-            cols = slice(block * P, (block + 1) * P)
-            grouped = stage.tile([P, P, PACK], BF16, name="grouped_wo%d" % block, align_bytes=64, offset=at)
+        def round_wo(first, count, at):
+            grouped = stage.tile([P, count, PACK], BF16, name="grouped_wo%d" % first, align_bytes=64, offset=at)
             nc.scalar.copy(
                 out=grouped[:].rearrange("p (c i) r -> p c r i", i=RUN),
-                in_=raw_wo[:, :, cols].rearrange("p r (c i) -> p c r i", i=RUN),
+                in_=raw_wo[:, :, first : first + count].rearrange("p r (c i) -> p c r i", i=RUN),
             )
-            return lambda: quantise(wo_codes[:, cols], wo_scales[:, cols], grouped[:].rearrange("p d r -> p (d r)"))
+            return grouped
 
-        prepare_wo(0, staged_at(last, 1) + 2 * WORD_BYTES * H)()
+        def quantise_wo(cols, grouped):
+            quantise(wo_codes[:, cols], wo_scales[:, cols], grouped.rearrange("p d r -> p (d r)"))
+
+        early_wo = round_wo(0, WO_EARLY, staged_at(last, 1) + 2 * WORD_BYTES * H)
+        quantise_wo(slice(0, P), early_wo[:, :P, :])
+        quantise_wo(slice(P, WO_EARLY), early_wo[:, P:, :])
 
         acts = []
         for q in range(QUARTERS):
@@ -195,7 +200,7 @@ def tile_attend_nsa_compress_kernel(tc, tok_words, tok_scales, w0, w1, w2, w3, g
             nc.scalar.activation(out=act[:], in_=z[q][:].rearrange("p t j -> p j t"), func=GELU)
             acts.append(act)
             if q == QUARTERS // 2 - 1:
-                quantise_second_block = prepare_wo(1, staged_at(2, 1))
+                late_wo = round_wo(WO_EARLY, D - WO_EARLY, staged_at(2, 1))
         g = [keep.tile([P, Q, PACK], BF16, name="g%d" % q, align_bytes=64) for q in range(QUARTERS)]
         g_mx = [mx_tiles("g%d" % q, Q) for q in range(QUARTERS)]
         for step in range(QUARTERS + 1):
@@ -204,7 +209,7 @@ def tile_attend_nsa_compress_kernel(tc, tok_words, tok_scales, w0, w1, w2, w3, g
             if step > 0:
                 quantise(g_mx[step - 1][0][:], g_mx[step - 1][1][:], g[step - 1][:].rearrange("p j t -> p (j t)"))
             if step == 1:
-                quantise_second_block()
+                quantise_wo(slice(WO_EARLY, D), late_wo[:])
 
         for q in range(QUARTERS):
             y = psum.tile([P, D // P, Q], F32, name="y%d" % q, tag="y%d" % q)

from contextlib import ExitStack

import concourse.mybir as mybir

K, T, J, F, D = 512, 2048, 512, 512, 256
P = 128
PACK = 4
PLACES = 4
LIST_ROWS = 16
SCALE_ROWS = 16
QUADRANT = 32
RUN = 4
QUARTERS = 4
Q = J // QUARTERS
H = J // 2
FLOPS = 2 * PLACES * K * F * J + 2 * F * D * J

F32 = mybir.dt.float32
BF16 = mybir.dt.bfloat16
I32 = mybir.dt.int32
U32 = mybir.dt.uint32
U16 = mybir.dt.uint16
U8 = mybir.dt.uint8
FP8X4 = mybir.dt.float8_e4m3fn_x4
FP4X4 = mybir.dt.float4_e2m1fn_x4
GELU = mybir.ActivationFunctionType.Gelu_apprx_tanh
MULT = mybir.AluOpType.mult
ADD = mybir.AluOpType.add

HALVES = (slice(0, F // 2), slice(F // 2, F))
HALF_BYTES = PACK * (F // 2) * 4
WORD_BYTES = 2
WO_EARLY = 3 * D // 4


def tile_attend_nsa_compress_kernel(tc, tok_words, tok_scales, w0, w1, w2, w3, gain, wo, offs, offs2, offs3, offs4, out):
    nc = tc.nc
    weights = (w0, w1, w2, w3)
    lists = (offs, offs2, offs3, offs4)
    last = PLACES - 1
    with ExitStack() as ctx:
        keep = ctx.enter_context(tc.tile_pool(name="keep", bufs=1))
        stage = ctx.enter_context(tc.tile_pool(name="stage", bufs=1))
        psum = ctx.enter_context(tc.psum_pool(name="psum", bufs=1))

        def staged_at(place, half):
            return (len(HALVES) * place + half) * HALF_BYTES

        raw = {}

        def load_half(place, half):
            tile = stage.tile([P, PACK, F // 2], F32, name="raw%d%d" % (place, half), align_bytes=64, offset=staged_at(place, half))
            nc.sync.dma_start(out=tile[:], in_=weights[place].rearrange("(p r) c -> p r c", r=PACK)[:, :, HALVES[half]])
            raw[place, half] = tile[:]

        def load_list(place):
            nc.sync.dma_start(offsets[place][:], lists[place])

        def mx_tiles(name, width):
            codes = keep.tile([P, width], U32, name=name + "_codes", align_bytes=64)
            scale_bytes = keep.tile([P, width], U8, name=name + "_scales", align_bytes=64)
            return codes, scale_bytes

        def quantise(codes, scale_bytes, values):
            nc.vector.quantize_mx(out=codes.bitcast(FP8X4), scales=scale_bytes, in_=values)

        pool_words = keep.tile([P, T], U16, name="pool_words", align_bytes=64)
        pool_scales = keep.tile([P, T], U8, name="pool_scales", align_bytes=64)
        offsets = [keep.tile([P, J // LIST_ROWS], U16, name="offsets%d" % place) for place in range(PLACES)]
        rows_in_quadrant = SCALE_ROWS * QUADRANT // P
        nc.vector.memset(pool_scales[:].bitcast(I32), 0)

        warm_in = keep.tile([P, 1], F32, name="warm_in")
        nc.gpsimd.memset(warm_in[:], 0.0)
        warm_out = keep.tile([P, 1], F32, name="warm_out")
        nc.scalar.activation(out=warm_out[:], in_=warm_in[:], func=GELU)

        nc.sync.dma_start(out=pool_words[:].bitcast(I32), in_=tok_words[0].bitcast(I32))
        load_list(0)
        load_list(1)
        for r in range(rows_in_quadrant):
            nc.sync.dma_start(
                out=pool_scales[r:P:QUADRANT, :].bitcast(I32),
                in_=tok_scales[0, r:SCALE_ROWS:rows_in_quadrant, :].bitcast(I32),
            )
        whole = stage.tile([P, PACK, F], F32, name="raw0", align_bytes=64, offset=staged_at(0, 0))
        nc.sync.dma_start(out=whole[:], in_=weights[0].rearrange("(p r) c -> p r c", r=PACK))
        for half, cols in enumerate(HALVES):
            raw[0, half] = whole[:, :, cols]
        load_half(1, 0)
        load_half(1, 1)
        for place in range(2, PLACES):
            load_list(place)
            for half in range(len(HALVES)):
                load_half(place, half)
        raw_wo = keep.tile([P, PACK, D], F32, name="raw_wo", align_bytes=64)
        nc.sync.dma_start(out=raw_wo[:], in_=wo.rearrange("(p r) c -> p r c", r=PACK))
        gains = keep.tile([P, PACK], F32, name="gains")
        nc.sync.dma_start(out=gains[:], in_=gain.rearrange("(p t) o -> p (t o)", t=PACK))

        dealt = [keep.tile([P, PACK, P, PACK], BF16, name="dealt%d" % place, align_bytes=64) for place in range(PLACES)]
        w_mx = [mx_tiles("w%d" % place, F) for place in range(PLACES)]
        z = [psum.tile([P, PACK, Q], F32, name="z%d" % q, tag="z%d" % q) for q in range(QUARTERS)]

        def gather(name, window, dtype, place, at=None, first=0, count=J):
            if at is None:
                picked = keep.tile([P, count], dtype, name=name, align_bytes=64)
            else:
                picked = stage.tile([P, count], dtype, name=name, align_bytes=64, offset=at)
            entries = offsets[place][:, first // LIST_ROWS : (first + count) // LIST_ROWS]
            nc.vector.tensor_copy(out=picked[:], in_=window[:].indirect(entries))
            return picked

        def cast_weights(place):
            for half, cols in enumerate(HALVES):
                m = slice(cols.start // PACK, cols.stop // PACK)
                if (place, half) == (0, 0):
                    nc.gpsimd.tensor_scalar(
                        out=dealt[place][:, :, m, :].rearrange("p t m r -> p m t r"),
                        in0=raw[place, half].rearrange("p r (m t) -> p m t r", t=PACK),
                        scalar1=1.0,
                        scalar2=0.0,
                        op0=MULT,
                        op1=ADD,
                    )
                    continue
                nc.scalar.copy(
                    out=dealt[place][:, :, m, :].rearrange("p t m r -> p m r t"),
                    in_=raw[place, half].rearrange("p r (m t) -> p m r t", t=PACK),
                )

        def quantise_weights(place):
            quantise(w_mx[place][0][:], w_mx[place][1][:], dealt[place][:].rearrange("p t m r -> p (t m r)"))

        words, scales = {}, {}

        def multiply(place, quarters):
            for n, q in enumerate(quarters):
                blocks = slice(n * Q, (n + 1) * Q)
                for t in range(PACK):
                    cols = slice(t * P, (t + 1) * P)
                    nc.tensor.matmul_mx(
                        out=z[q][:, t, :],
                        lhsT=w_mx[place][0][:, cols].bitcast(FP8X4),
                        lhsT_scale=w_mx[place][1][:, cols],
                        rhs=words[place][:, blocks].bitcast(FP4X4),
                        rhs_scale=scales[place][:, blocks],
                        start=(place == 0 and t == 0),
                        stop=(place == last and t == PACK - 1),
                    )

        for place in range(2):
            words[place] = gather("words%d" % place, pool_words, U16, place)
        for place in range(2):
            scales[place] = gather("scales%d" % place, pool_scales, U8, place)
        cast_weights(0)
        quantise_weights(0)
        multiply(0, range(QUARTERS))
        words[2] = gather("words2", pool_words, U16, 2, staged_at(0, 1))
        cast_weights(1)
        quantise_weights(1)
        multiply(1, range(QUARTERS))
        scales[2] = gather("scales2", pool_scales, U8, 2, staged_at(1, 1))
        cast_weights(2)
        quantise_weights(2)
        multiply(2, range(QUARTERS))
        words[last] = gather("words3low", pool_words, U16, last, staged_at(2, 1), 0, H)
        scales[last] = gather("scales3low", pool_scales, U8, last, staged_at(2, 1) + WORD_BYTES * H, 0, H)
        cast_weights(last)
        for half in range(len(HALVES)):
            for t in range(PACK):
                m = slice(half * P // 2, (half + 1) * P // 2)
                cols = slice(t * P + m.start, t * P + m.stop)
                quantise(w_mx[last][0][:, cols], w_mx[last][1][:, cols], dealt[last][:, t, m, :].rearrange("p m r -> p (m r)"))
        multiply(last, range(QUARTERS // 2))
        words[last] = gather("words3high", pool_words, U16, last, staged_at(last, 1), H, H)
        scales[last] = gather("scales3high", pool_scales, U8, last, staged_at(last, 1) + WORD_BYTES * H, H, H)
        multiply(last, range(QUARTERS // 2, QUARTERS))

        wo_codes, wo_scales = mx_tiles("wo", D)

        def round_wo(first, count, at):
            grouped = stage.tile([P, count, PACK], BF16, name="grouped_wo%d" % first, align_bytes=64, offset=at)
            nc.scalar.copy(
                out=grouped[:].rearrange("p (c i) r -> p c r i", i=RUN),
                in_=raw_wo[:, :, first : first + count].rearrange("p r (c i) -> p c r i", i=RUN),
            )
            return grouped

        def quantise_wo(cols, grouped):
            quantise(wo_codes[:, cols], wo_scales[:, cols], grouped.rearrange("p d r -> p (d r)"))

        early_wo = round_wo(0, WO_EARLY, staged_at(last, 1) + 2 * WORD_BYTES * H)
        quantise_wo(slice(0, P), early_wo[:, :P, :])
        quantise_wo(slice(P, WO_EARLY), early_wo[:, P:, :])

        acts = []
        for q in range(QUARTERS):
            act = keep.tile([P, Q, PACK], F32, name="act%d" % q, align_bytes=64)
            nc.scalar.activation(out=act[:], in_=z[q][:].rearrange("p t j -> p j t"), func=GELU)
            acts.append(act)
            if q == QUARTERS // 2 - 1:
                late_wo = round_wo(WO_EARLY, D - WO_EARLY, staged_at(2, 1))
        g = [keep.tile([P, Q, PACK], BF16, name="g%d" % q, align_bytes=64) for q in range(QUARTERS)]
        g_mx = [mx_tiles("g%d" % q, Q) for q in range(QUARTERS)]
        for step in range(QUARTERS + 1):
            if step < QUARTERS:
                nc.vector.tensor_tensor(out=g[step][:], in0=acts[step][:], in1=gains[:].unsqueeze(1).to_broadcast([P, Q, PACK]), op=MULT)
            if step > 0:
                quantise(g_mx[step - 1][0][:], g_mx[step - 1][1][:], g[step - 1][:].rearrange("p j t -> p (j t)"))
            if step == 1:
                quantise_wo(slice(WO_EARLY, D), late_wo[:])

        for q in range(QUARTERS):
            y = psum.tile([P, D // P, Q], F32, name="y%d" % q, tag="y%d" % q)
            for block in range(D // P):
                rows = slice(block * P, (block + 1) * P)
                nc.tensor.matmul_mx(
                    out=y[:, block, :],
                    lhsT=wo_codes[:, rows].bitcast(FP8X4),
                    lhsT_scale=wo_scales[:, rows],
                    rhs=g_mx[q][0][:].bitcast(FP8X4),
                    rhs_scale=g_mx[q][1][:],
                    start=True,
                    stop=True,
                )
            result = keep.tile([P, D // P, Q], F32, name="result%d" % q, align_bytes=64)
            copy = nc.vector.tensor_copy if q == QUARTERS - 1 else nc.scalar.copy
            copy(out=result[:], in_=y[:])
            nc.sync.dma_start(out=out.rearrange("(b p) j -> p b j", p=P)[:, :, q * Q : (q + 1) * Q], in_=result[:])
